import numpy as np
import ml_dtypes


def mxq(x, axis, fmt="e4m3"):
    dtype, down = {"e4m3": (ml_dtypes.float8_e4m3fn, 7), "e5m2": (ml_dtypes.float8_e5m2, 14)}[fmt]
    v = np.moveaxis(np.asarray(x, np.float32).astype(ml_dtypes.bfloat16).astype(np.float64), axis, -1)
    blocks = v.reshape(v.shape[:-1] + (-1, 32))
    amax = np.abs(blocks).max(-1, keepdims=True)
    byte = np.maximum(np.where(amax > 0, np.frexp(amax)[1] - 1 + 127, 0) - down, 1)
    scale = np.exp2(byte - 127.0)
    codes = (blocks / scale).astype(np.float32).astype(dtype).astype(np.float64)
    return np.moveaxis((codes * scale).reshape(v.shape), -1, axis)


WIDE = False


def mx_kscale(k):
    if not WIDE:
        return np.ones(k)
    levels = np.array([10, -10, 5, -5, 0])
    if k % 512:
        return np.exp2(np.random.permutation(np.resize(levels, k // 32))).repeat(32)
    a = np.empty((k // 512, 16))
    for p in range(k // 512):
        a[p, :8] = np.random.permutation(np.resize(levels, 8))
        for g in range(8):
            far = levels[np.abs(levels - a[p, g]) >= 10]
            a[p, g + 8] = far[np.random.randint(len(far))]
    return np.exp2(a.ravel()).repeat(32)


def f64(x):
    return np.asarray(x).astype(np.float64)


def striped(idx):
    return np.tile(np.asarray(idx).reshape(-1, 16).T, (8, 1)).astype(np.uint16)


def unstriped(offs):
    return offs[:16].T.reshape(-1).astype(np.int64)


E2M1 = np.array([0.0, 0.5, 1.0, 1.5, 2.0, 3.0, 4.0, 6.0, -0.0, -0.5, -1.0, -1.5, -2.0, -3.0, -4.0, -6.0])


def pack_weight(w, fmt):
    k, n = w.shape
    w = f64(np.asarray(w, np.float32).astype(ml_dtypes.bfloat16)).reshape(k // 32, 32, n)
    amax = np.abs(w).max(1)
    if fmt == "e4m3":
        byte = np.frexp(amax)[1] - 1 + 127 - 7
    else:
        mant, ex = np.frexp(amax / 6.0)
        byte = np.where(mant > 0.5, ex, ex - 1) + 127
    byte = np.clip(np.where(amax > 0, byte, 1), 1, 254)
    scaled = (w * np.exp2(127.0 - byte)[:, None, :]).reshape(k, n).astype(np.float32)
    by_word = np.ascontiguousarray(scaled.reshape(k // 512, 128, 4, n).transpose(0, 1, 3, 2))
    if fmt == "e4m3":
        words = by_word.astype(ml_dtypes.float8_e4m3fn).view(np.uint8)
    else:
        c = by_word.astype(ml_dtypes.float4_e2m1fn).view(np.uint8) & 0xF
        words = (c[..., 0::2] | (c[..., 1::2] << 4)).reshape(k // 512, 128, 2 * n)
    return np.ascontiguousarray(words), np.ascontiguousarray(byte.astype(np.uint8).reshape(k // 512, 16, n))


def unpack_weight(words, scales, fmt):
    g, _, n = scales.shape
    words = np.ascontiguousarray(words).reshape(g, 128, n, -1)
    if fmt == "e4m3":
        vals = words.view(ml_dtypes.float8_e4m3fn).astype(np.float64)
    else:
        nib = np.empty((g, 128, n, 4), np.uint8)
        nib[..., 0::2] = words & 0xF
        nib[..., 1::2] = words >> 4
        vals = E2M1[nib]
    vals = vals * np.repeat(np.exp2(scales.astype(np.float64) - 127.0), 8, axis=1)[..., None]
    return vals.transpose(0, 1, 3, 2).reshape(g * 512, n)


def bf(x):
    return np.asarray(x, np.float32).astype(ml_dtypes.bfloat16)


def planes(Y):
    r, m = Y.shape
    b = f64(bf(Y)).reshape(r // 32, 32, m)
    amax = np.abs(b).max(1)
    byte = np.clip(np.where(amax > 0, np.frexp(amax)[1] - 1 + 127 - 7, 1), 1, 254)
    codes = (b * np.exp2(127.0 - byte)[:, None, :]).reshape(r, m).astype(np.float32).astype(ml_dtypes.float8_e4m3fn).view(np.uint8)
    words = codes.reshape(r // 512, 128, 4, m).transpose(0, 1, 3, 2)
    return np.ascontiguousarray(words), np.ascontiguousarray(byte.astype(np.uint8).reshape(r // 512, 16, m))


D, C, T, I, Q, E = 512, 1024, 2048, 512, 256, 512


def setup_inputs():
    n = np.random.standard_normal
    idx = np.random.randint(0, C, I)
    idx2 = np.random.permutation(T)[:I]
    fd = mx_kscale(D)
    fi = mx_kscale(I)
    ti = np.ones(T)
    ti[idx2] = fi
    bookp = pack_weight(n((D, C)) / fd[:, None], "e2m1")
    return {
        "query": (n((D, Q)) * 0.5 / np.sqrt(D) * fd[:, None]).astype(np.float32),
        "book_words": bookp[0],
        "book_scales": bookp[1],
        "size": (np.random.uniform(0.5, 2.0, (1, I)) * fi).astype(np.float32),
        "vals": (n((E, T)) / ti).astype(np.float32),
        "offs": striped(idx),
        "offs2": striped(idx2),
    }


def reference(query, book_words, book_scales, size, vals, offs, offs2):
    idx = unstriped(offs)
    idx2 = unstriped(offs2)
    booku = unpack_weight(book_words, book_scales, "e2m1")
    queryq = mxq(f64(query), 0, "e4m3")
    b = queryq.T @ booku
    p = np.exp(b[:, idx] - np.max(b[:, idx], axis=1, keepdims=True))
    w = p * f64(size) / np.sum(p, axis=1, keepdims=True)
    wt = w.T
    vt = f64(vals)[:, idx2].T
    vtq = mxq(vt, 0, "e4m3")
    wtq = mxq(wt, 0, "e4m3")
    o = vtq.T @ wtq
    words, scales = planes(o)
    return o, words, scales

@@ -1,0 +1,218 @@
+from contextlib import ExitStack
+
+import concourse.mybir as mybir
+from concourse.masks import make_identity
+
+D, C, T, I, Q, E = 512, 1024, 2048, 512, 256, 512
+FLOPS = 2 * D * Q * C + 2 * I * E * Q
+
+F32 = mybir.dt.float32
+BF16 = mybir.dt.bfloat16
+I32 = mybir.dt.int32
+U32 = mybir.dt.uint32
+U16 = mybir.dt.uint16
+U8 = mybir.dt.uint8
+FP8X4 = mybir.dt.float8_e4m3fn_x4
+FP4X4 = mybir.dt.float4_e2m1fn_x4
+ACT = mybir.ActivationFunctionType
+ALU = mybir.AluOpType
+AXIS = mybir.AxisListType
+
+P = 128
+PACK = 4
+BANK = 512
+HALVES = Q // P
+
+
+def tile_attend_vqattention_pl_kernel(tc, query, book_words, book_scales, size, vals, offs, offs2, out_0, out_1, out_2):
+    nc = tc.nc
+    with ExitStack() as ctx:
+        sb = ctx.enter_context(tc.tile_pool(name="sb", bufs=1))
+        ps = ctx.enter_context(tc.psum_pool(name="ps", bufs=1))
+
+        def sbuf(name, shape, dtype, tag=None):
+            return sb.tile(shape, dtype, name=name, tag=tag or name, align_bytes=64)
+
+        banks = [ps.tile([P, BANK], F32, name="bank%d" % n) for n in range(8)]
+
+        query_rows = query.rearrange("(p j) q -> p j q", j=PACK)
+        query_raw = [sbuf("query_raw%d" % h, [P, PACK, P], F32) for h in range(HALVES)]
+        book_plane = sbuf("book_plane", [P, C], U8)
+        book_codes = sbuf("book_codes", [P, 2 * C], U8)
+        nc.sync.dma_start(out=query_raw[0][:], in_=query_rows[:, :, :P])
+        nc.sync.dma_start(out=book_codes[:].bitcast(I32), in_=book_words[0].bitcast(I32))
+        for quad, queue in enumerate([nc.sync, nc.scalar, nc.sync, nc.scalar]):
+            queue.dma_start(
+                out=book_plane[32 * quad : 32 * quad + 4, :].bitcast(I32),
+                in_=book_scales[0, 4 * quad : 4 * quad + 4, :].bitcast(I32),
+            )
+        nc.sync.dma_start(out=query_raw[1][:], in_=query_rows[:, :, P:])
+        code_list = sbuf("code_list", [P, I // 16], U16)
+        vals_rows = vals.rearrange("(m t) n -> t m n", t=PACK)
+        pools = [sbuf("pool%d" % t, [P, T], F32) for t in range(PACK)]
+        nc.sync.dma_start(out=pools[0][:], in_=vals_rows[0])
+        nc.sync.dma_start(code_list[:], offs)
+        size_cols = sbuf("size_cols", [P, PACK], F32)
+        nc.sync.dma_start(out=size_cols[:], in_=size.rearrange("o (s r) -> (o s) r", r=PACK))
+        token_list = sbuf("token_list", [P, I // 16], U16)
+        nc.sync.dma_start(token_list[:], offs2)
+        for t in range(1, PACK):
+            nc.sync.dma_start(out=pools[t][:], in_=vals_rows[t])
+
+        zero = sbuf("zero", [P, 1], F32)
+        nc.vector.memset(zero[:], 0.0)
+        warm = sbuf("warm", [P, 1], F32)
+        nc.scalar.activation(warm[:], zero[:], ACT.Exp)
+        ident = sbuf("ident", [P, P], F32)
+        make_identity(nc, ident[:])
+
+        q_codes, q_planes = [], []
+        q_grouped = [sbuf("q_grouped%d" % h, [P, P, PACK], BF16) for h in range(HALVES)]
+        for h in range(HALVES):
+            src = query_raw[h][:].rearrange("p j q -> p q j")
+            if h == 0:
+                nc.vector.tensor_copy(q_grouped[h][:], src)
+            else:
+                nc.scalar.copy(q_grouped[h][:], src)
+        for h in range(HALVES):
+            codes = sbuf("q_codes%d" % h, [P, P], U32)
+            plane = sbuf("q_plane%d" % h, [P, P], U8)
+            nc.vector.quantize_mx(out=codes[:].bitcast(FP8X4), scales=plane[:], in_=q_grouped[h][:].rearrange("p q j -> p (q j)"))
+            q_codes.append(codes)
+            q_planes.append(plane)
+
+        scores = [sbuf("scores%d" % h, [P, C], F32) for h in range(HALVES)]
+        pieces = [(0, n * 256, 256) for n in range(4)] + [(1, n * BANK, BANK) for n in range(2)]
+        for n, (h, first, width) in enumerate(pieces):
+            nc.tensor.matmul_mx(
+                out=banks[n][:, :width],
+                lhsT=q_codes[h][:].bitcast(FP8X4),
+                lhsT_scale=q_planes[h][:],
+                rhs=book_codes[:, 2 * first : 2 * (first + width)].bitcast(FP4X4),
+                rhs_scale=book_plane[:, first : first + width],
+                start=True,
+                stop=True,
+            )
+        size_bank = banks[0]
+        for n, (h, first, width) in enumerate(pieces):
+            copy = nc.vector.tensor_copy if h == 0 and n % 2 == 1 else nc.scalar.copy
+            copy(scores[h][:, first : first + width], banks[n][:, :width])
+        for r in range(PACK):
+            nc.tensor.transpose(size_bank[:, r * P : (r + 1) * P], size_cols[:, r : r + 1].to_broadcast([P, P]), ident[:])
+
+        picked = sbuf("picked", [P, HALVES, I], F32)
+        probs = {}
+        neg_max = [sbuf("neg_max%d" % h, [P, 1], F32) for h in range(HALVES)]
+        total = [sbuf("total%d" % h, [P, 1], F32) for h in range(HALVES)]
+        inv_total = [sbuf("inv_total%d" % h, [P, 1], F32) for h in range(HALVES)]
+        gathered = {}
+
+        def gather_values(t, reused):
+            gathered[t] = sbuf("gathered%d" % t, [P, I], BF16, tag=reused)
+            nc.vector.tensor_copy(gathered[t][:], pools[t][:].indirect(token_list[:]))
+
+        pool0_bf16 = sbuf("pool0_bf16", [P, T], BF16, tag="size_cols")
+        nc.scalar.activation(pool0_bf16[:], pools[0][:], ACT.Copy)
+        for h in range(HALVES):
+            nc.vector.tensor_copy(picked[:, h, :], scores[h][:].indirect(code_list[:]))
+        for h, reused in enumerate(["scores1", "scores0"]):
+            negated = sbuf("negated%d" % h, [P, I], BF16, tag=reused)
+            nc.vector.tensor_scalar(negated[:], picked[:, h, :], -1.0, None, ALU.mult, ALU.min, accum_out=neg_max[h][:])
+        for h, reused in enumerate(["pool0", None]):
+            probs[h] = sbuf("probs%d" % h, [P, I], F32, tag=reused)
+            nc.scalar.activation(probs[h][:], picked[:, h, :], ACT.Exp, bias=neg_max[h][:], accum_out=total[h][:])
+        gathered[0] = sbuf("gathered0", [P, I], BF16, tag="picked")
+        nc.scalar.activation(gathered[0][:], pool0_bf16[:].indirect(token_list[:]), ACT.Copy)
+        gather_values(1, "scores0")
+        weights = [sbuf("weights0", [P, I], BF16), sbuf("weights1", [P, I], BF16, tag="pool1")]
+        for h in range(HALVES):
+            nc.vector.reciprocal(inv_total[h][:], total[h][:])
+            nc.vector.scalar_tensor_tensor(
+                weights[h][:].rearrange("p (s r) -> p s r", r=PACK),
+                probs[h][:].rearrange("p (s r) -> p s r", r=PACK),
+                inv_total[h][:],
+                size_bank[:].rearrange("p (r s) -> p s r", r=PACK),
+                ALU.mult,
+                ALU.mult,
+            )
+
+        def turn(src, bank, dst):
+            words = src[:].bitcast(F32)
+            for u in range(2):
+                nc.tensor.transpose(bank[:, u * P : (u + 1) * P], words[:, u : I // 2 : 2], ident[:])
+            nc.scalar.copy(dst.bitcast(F32).rearrange("p (m u) -> p m u", u=2), bank[:, : 2 * P].rearrange("p (u m) -> p m u", u=2))
+
+        out_banks = [banks[5], banks[7]]
+
+        def multiply(t, codes, plane):
+            for h in range(HALVES):
+                nc.tensor.matmul_mx(
+                    out=out_banks[h][:, t * P : (t + 1) * P],
+                    lhsT=codes.bitcast(FP8X4),
+                    lhsT_scale=plane,
+                    rhs=w_codes[:, h * P : (h + 1) * P].bitcast(FP8X4),
+                    rhs_scale=w_plane[:, h * P : (h + 1) * P],
+                    start=True,
+                    stop=True,
+                )
+
+        def quantize_values(tiles, grouped, reused=None):
+            width = len(tiles) * P
+            codes = sbuf("v_codes%d" % tiles[0], [P, width], U32, tag=reused)
+            plane = sbuf("v_plane%d" % tiles[0], [P, width], U8)
+            nc.vector.quantize_mx(out=codes[:].bitcast(FP8X4), scales=plane[:], in_=grouped[:])
+            for n, t in enumerate(tiles):
+                multiply(t, codes[:, n * P : (n + 1) * P], plane[:, n * P : (n + 1) * P])
+
+        v_grouped01 = sbuf("v_grouped01", [P, 2 * I], BF16, tag="size_cols")
+        w_grouped = sbuf("w_grouped", [P, Q * PACK], BF16)
+        turn(gathered[1], banks[2], v_grouped01[:, I:])
+        for h in range(HALVES):
+            turn(weights[h], banks[1 if h == 0 else 6], w_grouped[:, h * I : (h + 1) * I])
+        turn(gathered[0], banks[3], v_grouped01[:, :I])
+        gather_values(2, "probs1")
+        v_grouped2 = sbuf("v_grouped2", [P, I], BF16)
+        turn(gathered[2], banks[4], v_grouped2[:])
+        w_codes = sbuf("w_codes", [P, Q], U32)
+        w_plane = sbuf("w_plane", [P, Q], U8)
+        nc.vector.quantize_mx(out=w_codes[:].bitcast(FP8X4), scales=w_plane[:], in_=w_grouped[:])
+        quantize_values([0, 1], v_grouped01, "pool2")
+        gather_values(3, "w_grouped")
+        result = sbuf("result", [P, PACK, Q], F32)
+        out_rows = out_0.rearrange("(m t) q -> m t q", t=PACK)
+
+        def copy_out(first):
+            for h in range(HALVES):
+                nc.scalar.copy(
+                    result[:, first : first + 2, h * P : (h + 1) * P],
+                    out_banks[h][:, first * P : (first + 2) * P].rearrange("p (t q) -> p t q", t=2),
+                )
+
+        copy_out(0)
+        nc.sync.dma_start(out=out_rows[:, :2, :], in_=result[:, :2, :])
+        quantize_values([2], v_grouped2, "pool3")
+        v_grouped3 = sbuf("v_grouped3", [P, I], BF16)
+        turn(gathered[3], banks[2], v_grouped3[:])
+        quantize_values([3], v_grouped3)
+
+        o_grouped = [sbuf("o_grouped%d" % h, [P, P, PACK], BF16) for h in range(HALVES)]
+        o_codes = sbuf("o_codes", [P, Q], U32)
+        o_plane = sbuf("o_plane", [P, Q], U8)
+        for h in range(HALVES):
+            copy = nc.vector.tensor_copy if h == 0 else nc.scalar.copy
+            copy(o_grouped[h][:], out_banks[h][:].rearrange("p (t q) -> p q t", t=PACK))
+        for h in range(HALVES):
+            nc.vector.quantize_mx(
+                out=o_codes[:, h * P : (h + 1) * P].bitcast(FP8X4),
+                scales=o_plane[:, h * P : (h + 1) * P],
+                in_=o_grouped[h][:].rearrange("p q t -> p (q t)"),
+            )
+        copy_out(2)
+        nc.scalar.dma_start(out=out_rows[:, 2:, :], in_=result[:, 2:, :])
+        nc.sync.dma_start(out=out_1[0].rearrange("p c r -> p (c r)").bitcast(I32), in_=o_codes[:].bitcast(I32))
+        for quad in range(4):
+            queue = nc.sync if quad % 2 == 0 else nc.scalar
+            queue.dma_start(
+                out=out_2[0, 4 * quad : 4 * quad + 4, :].bitcast(I32),
+                in_=o_plane[32 * quad : 32 * quad + 4, :].bitcast(I32),
+            )

@@ -35,23 +35,21 @@ def tile_attend_vqattention_pl_kernel(tc, query, book_words, book_scales, size, 
 
         banks = [ps.tile([P, BANK], F32, name="bank%d" % n) for n in range(8)]
 
-        query_rows = query.rearrange("(p j) q -> p j q", j=PACK)
-        query_raw = [sbuf("query_raw%d" % h, [P, PACK, P], F32) for h in range(HALVES)]
+        query_raw = sbuf("query_raw", [P, PACK, Q], F32)
         book_plane = sbuf("book_plane", [P, C], U8)
         book_codes = sbuf("book_codes", [P, 2 * C], U8)
-        nc.sync.dma_start(out=query_raw[0][:], in_=query_rows[:, :, :P])
+        nc.sync.dma_start(out=query_raw[:], in_=query.rearrange("(p j) q -> p j q", j=PACK))
         nc.sync.dma_start(out=book_codes[:].bitcast(I32), in_=book_words[0].bitcast(I32))
-        for quad, queue in enumerate([nc.sync, nc.scalar, nc.sync, nc.scalar]):
+        for quad, queue in enumerate([nc.scalar, nc.scalar, nc.sync, nc.scalar]):
             queue.dma_start(
                 out=book_plane[32 * quad : 32 * quad + 4, :].bitcast(I32),
                 in_=book_scales[0, 4 * quad : 4 * quad + 4, :].bitcast(I32),
             )
-        nc.sync.dma_start(out=query_raw[1][:], in_=query_rows[:, :, P:])
         code_list = sbuf("code_list", [P, I // 16], U16)
+        nc.sync.dma_start(code_list[:], offs)
         vals_rows = vals.rearrange("(m t) n -> t m n", t=PACK)
         pools = [sbuf("pool%d" % t, [P, T], F32) for t in range(PACK)]
         nc.sync.dma_start(out=pools[0][:], in_=vals_rows[0])
-        nc.sync.dma_start(code_list[:], offs)
         size_cols = sbuf("size_cols", [P, PACK], F32)
         nc.sync.dma_start(out=size_cols[:], in_=size.rearrange("o (s r) -> (o s) r", r=PACK))
         token_list = sbuf("token_list", [P, I // 16], U16)
@@ -69,7 +67,7 @@ def tile_attend_vqattention_pl_kernel(tc, query, book_words, book_scales, size, 
         q_codes, q_planes = [], []
         q_grouped = [sbuf("q_grouped%d" % h, [P, P, PACK], BF16) for h in range(HALVES)]
         for h in range(HALVES):
-            src = query_raw[h][:].rearrange("p j q -> p q j")
+            src = query_raw[:, :, h * P : (h + 1) * P].rearrange("p j q -> p q j")
             if h == 0:
                 nc.vector.tensor_copy(q_grouped[h][:], src)
             else:
@@ -93,15 +91,15 @@ def tile_attend_vqattention_pl_kernel(tc, query, book_words, book_scales, size, 
                 start=True,
                 stop=True,
             )
-        size_bank = banks[0]
+        size_bank = banks[4]
         for n, (h, first, width) in enumerate(pieces):
             copy = nc.vector.tensor_copy if h == 0 and n % 2 == 1 else nc.scalar.copy
             copy(scores[h][:, first : first + width], banks[n][:, :width])
         for r in range(PACK):
             nc.tensor.transpose(size_bank[:, r * P : (r + 1) * P], size_cols[:, r : r + 1].to_broadcast([P, P]), ident[:])
 
-        picked = sbuf("picked", [P, HALVES, I], F32)
-        probs = {}
+        picked = sbuf("picked", [P, HALVES, I], F32, tag="q_grouped1")
+
         neg_max = [sbuf("neg_max%d" % h, [P, 1], F32) for h in range(HALVES)]
         total = [sbuf("total%d" % h, [P, 1], F32) for h in range(HALVES)]
         inv_total = [sbuf("inv_total%d" % h, [P, 1], F32) for h in range(HALVES)]
@@ -118,23 +116,26 @@ def tile_attend_vqattention_pl_kernel(tc, query, book_words, book_scales, size, 
         for h, reused in enumerate(["scores1", "scores0"]):
             negated = sbuf("negated%d" % h, [P, I], BF16, tag=reused)
             nc.vector.tensor_scalar(negated[:], picked[:, h, :], -1.0, None, ALU.mult, ALU.min, accum_out=neg_max[h][:])
-        for h, reused in enumerate(["pool0", None]):
-            probs[h] = sbuf("probs%d" % h, [P, I], F32, tag=reused)
-            nc.scalar.activation(probs[h][:], picked[:, h, :], ACT.Exp, bias=neg_max[h][:], accum_out=total[h][:])
-        gathered[0] = sbuf("gathered0", [P, I], BF16, tag="picked")
+        probs = sbuf("probs", [P, HALVES, I], F32, tag="pool0")
+        for h in range(HALVES):
+            nc.scalar.activation(probs[:, h, :], picked[:, h, :], ACT.Exp, bias=neg_max[h][:], accum_out=total[h][:])
+        gathered[0] = sbuf("gathered0", [P, I], BF16, tag="q_grouped1")
         nc.scalar.activation(gathered[0][:], pool0_bf16[:].indirect(token_list[:]), ACT.Copy)
         gather_values(1, "scores0")
         weights = [sbuf("weights0", [P, I], BF16), sbuf("weights1", [P, I], BF16, tag="pool1")]
         for h in range(HALVES):
             nc.vector.reciprocal(inv_total[h][:], total[h][:])
+        for h in range(HALVES):
             nc.vector.scalar_tensor_tensor(
                 weights[h][:].rearrange("p (s r) -> p s r", r=PACK),
-                probs[h][:].rearrange("p (s r) -> p s r", r=PACK),
+                probs[:, h, :].rearrange("p (s r) -> p s r", r=PACK),
                 inv_total[h][:],
                 size_bank[:].rearrange("p (r s) -> p s r", r=PACK),
                 ALU.mult,
                 ALU.mult,
             )
+        gather_values(2, "inv_total0")
+        gather_values(3, "inv_total1")
 
         def turn(src, bank, dst):
             words = src[:].bitcast(F32)
@@ -142,58 +143,49 @@ def tile_attend_vqattention_pl_kernel(tc, query, book_words, book_scales, size, 
                 nc.tensor.transpose(bank[:, u * P : (u + 1) * P], words[:, u : I // 2 : 2], ident[:])
             nc.scalar.copy(dst.bitcast(F32).rearrange("p (m u) -> p m u", u=2), bank[:, : 2 * P].rearrange("p (u m) -> p m u", u=2))
 
-        out_banks = [banks[5], banks[7]]
-
-        def multiply(t, codes, plane):
-            for h in range(HALVES):
-                nc.tensor.matmul_mx(
-                    out=out_banks[h][:, t * P : (t + 1) * P],
-                    lhsT=codes.bitcast(FP8X4),
-                    lhsT_scale=plane,
-                    rhs=w_codes[:, h * P : (h + 1) * P].bitcast(FP8X4),
-                    rhs_scale=w_plane[:, h * P : (h + 1) * P],
-                    start=True,
-                    stop=True,
-                )
-
-        def quantize_values(tiles, grouped, reused=None):
-            width = len(tiles) * P
-            codes = sbuf("v_codes%d" % tiles[0], [P, width], U32, tag=reused)
-            plane = sbuf("v_plane%d" % tiles[0], [P, width], U8)
-            nc.vector.quantize_mx(out=codes[:].bitcast(FP8X4), scales=plane[:], in_=grouped[:])
-            for n, t in enumerate(tiles):
-                multiply(t, codes[:, n * P : (n + 1) * P], plane[:, n * P : (n + 1) * P])
-
-        v_grouped01 = sbuf("v_grouped01", [P, 2 * I], BF16, tag="size_cols")
-        w_grouped = sbuf("w_grouped", [P, Q * PACK], BF16)
-        turn(gathered[1], banks[2], v_grouped01[:, I:])
+        early = sbuf("early", [P, 4 * I], BF16, tag="size_cols")
         for h in range(HALVES):
-            turn(weights[h], banks[1 if h == 0 else 6], w_grouped[:, h * I : (h + 1) * I])
-        turn(gathered[0], banks[3], v_grouped01[:, :I])
-        gather_values(2, "probs1")
-        v_grouped2 = sbuf("v_grouped2", [P, I], BF16)
-        turn(gathered[2], banks[4], v_grouped2[:])
-        w_codes = sbuf("w_codes", [P, Q], U32)
-        w_plane = sbuf("w_plane", [P, Q], U8)
-        nc.vector.quantize_mx(out=w_codes[:].bitcast(FP8X4), scales=w_plane[:], in_=w_grouped[:])
-        quantize_values([0, 1], v_grouped01, "pool2")
-        gather_values(3, "w_grouped")
+            turn(weights[h], banks[1 if h == 0 else 6], early[:, h * I : (h + 1) * I])
+        turn(gathered[1], size_bank, early[:, 3 * I :])
+        turn(gathered[0], banks[3], early[:, 2 * I : 3 * I])
+        late = sbuf("late", [P, 2 * I], BF16)
+        turn(gathered[2], banks[0], late[:, :I])
+        turn(gathered[3], banks[2], late[:, I:])
+        early_codes = sbuf("early_codes", [P, 4 * P], U32, tag="pool3")
+        early_plane = sbuf("early_plane", [P, 4 * P], U8)
+        nc.vector.quantize_mx(out=early_codes[:].bitcast(FP8X4), scales=early_plane[:], in_=early[:])
+        late_codes = sbuf("late_codes", [P, 2 * P], U32)
+        late_plane = sbuf("late_plane", [P, 2 * P], U8)
+        nc.vector.quantize_mx(out=late_codes[:].bitcast(FP8X4), scales=late_plane[:], in_=late[:])
+
+        out_banks = [banks[5], banks[7]]
         result = sbuf("result", [P, PACK, Q], F32)
         out_rows = out_0.rearrange("(m t) q -> m t q", t=PACK)
 
-        def copy_out(first):
+        def multiply(first, codes, plane):
             for h in range(HALVES):
-                nc.scalar.copy(
-                    result[:, first : first + 2, h * P : (h + 1) * P],
-                    out_banks[h][:, first * P : (first + 2) * P].rearrange("p (t q) -> p t q", t=2),
-                )
+                for n in range(2):
+                    nc.tensor.matmul_mx(
+                        out=out_banks[h][:, (first + n) * P : (first + n + 1) * P],
+                        lhsT=codes[:, n * P : (n + 1) * P].bitcast(FP8X4),
+                        lhsT_scale=plane[:, n * P : (n + 1) * P],
+                        rhs=early_codes[:, h * P : (h + 1) * P].bitcast(FP8X4),
+                        rhs_scale=early_plane[:, h * P : (h + 1) * P],
+                        start=True,
+                        stop=True,
+                    )
 
-        copy_out(0)
+        def copy_out(first, h, copy):
+            copy(
+                result[:, first : first + 2, h * P : (h + 1) * P],
+                out_banks[h][:, first * P : (first + 2) * P].rearrange("p (t q) -> p t q", t=2),
+            )
+
+        multiply(0, early_codes[:, 2 * P :], early_plane[:, 2 * P :])
+        copy_out(0, 0, nc.scalar.copy)
+        copy_out(0, 1, nc.scalar.copy)
         nc.sync.dma_start(out=out_rows[:, :2, :], in_=result[:, :2, :])
-        quantize_values([2], v_grouped2, "pool3")
-        v_grouped3 = sbuf("v_grouped3", [P, I], BF16)
-        turn(gathered[3], banks[2], v_grouped3[:])
-        quantize_values([3], v_grouped3)
+        multiply(2, late_codes[:], late_plane[:])
 
         o_grouped = [sbuf("o_grouped%d" % h, [P, P, PACK], BF16) for h in range(HALVES)]
         o_codes = sbuf("o_codes", [P, Q], U32)
@@ -207,11 +199,12 @@ def tile_attend_vqattention_pl_kernel(tc, query, book_words, book_scales, size, 
                 scales=o_plane[:, h * P : (h + 1) * P],
                 in_=o_grouped[h][:].rearrange("p q t -> p (q t)"),
             )
-        copy_out(2)
+        for h in range(HALVES):
+            copy_out(2, h, nc.scalar.copy)
         nc.scalar.dma_start(out=out_rows[:, 2:, :], in_=result[:, 2:, :])
         nc.sync.dma_start(out=out_1[0].rearrange("p c r -> p (c r)").bitcast(I32), in_=o_codes[:].bitcast(I32))
         for quad in range(4):
-            queue = nc.sync if quad % 2 == 0 else nc.scalar
+            queue = nc.sync if quad != 3 else nc.scalar
             queue.dma_start(
                 out=out_2[0, 4 * quad : 4 * quad + 4, :].bitcast(I32),
                 in_=o_plane[32 * quad : 32 * quad + 4, :].bitcast(I32),

@@ -45,11 +45,13 @@ def tile_attend_vqattention_pl_kernel(tc, query, book_words, book_scales, size, 
                 out=book_plane[32 * quad : 32 * quad + 4, :].bitcast(I32),
                 in_=book_scales[0, 4 * quad : 4 * quad + 4, :].bitcast(I32),
             )
+        vals_rows = vals.rearrange("(m t) n -> t m n", t=PACK)
+        pool0_parts = [sbuf("pool0_part%d" % n, [P, T // 2], F32) for n in range(2)]
+        pools = {t: sbuf("pool%d" % t, [P, T], F32) for t in range(1, PACK)}
+        for n in range(2):
+            nc.sync.dma_start(out=pool0_parts[n][:], in_=vals_rows[0][:, n * T // 2 : (n + 1) * T // 2])
         code_list = sbuf("code_list", [P, I // 16], U16)
         nc.sync.dma_start(code_list[:], offs)
-        vals_rows = vals.rearrange("(m t) n -> t m n", t=PACK)
-        pools = [sbuf("pool%d" % t, [P, T], F32) for t in range(PACK)]
-        nc.sync.dma_start(out=pools[0][:], in_=vals_rows[0])
         size_cols = sbuf("size_cols", [P, PACK], F32)
         nc.sync.dma_start(out=size_cols[:], in_=size.rearrange("o (s r) -> (o s) r", r=PACK))
         token_list = sbuf("token_list", [P, I // 16], U16)
@@ -66,12 +68,10 @@ def tile_attend_vqattention_pl_kernel(tc, query, book_words, book_scales, size, 
 
         q_codes, q_planes = [], []
         q_grouped = [sbuf("q_grouped%d" % h, [P, P, PACK], BF16) for h in range(HALVES)]
-        for h in range(HALVES):
-            src = query_raw[:, :, h * P : (h + 1) * P].rearrange("p j q -> p q j")
-            if h == 0:
-                nc.vector.tensor_copy(q_grouped[h][:], src)
-            else:
-                nc.scalar.copy(q_grouped[h][:], src)
+        by_query = query_raw[:].rearrange("p j q -> p q j")
+        nc.vector.tensor_copy(q_grouped[0][:, : P // 2, :], by_query[:, : P // 2, :])
+        nc.scalar.copy(q_grouped[0][:, P // 2 :, :], by_query[:, P // 2 : P, :])
+        nc.scalar.copy(q_grouped[1][:], by_query[:, P:, :])
         for h in range(HALVES):
             codes = sbuf("q_codes%d" % h, [P, P], U32)
             plane = sbuf("q_plane%d" % h, [P, P], U8)
@@ -80,7 +80,7 @@ def tile_attend_vqattention_pl_kernel(tc, query, book_words, book_scales, size, 
             q_planes.append(plane)
 
         scores = [sbuf("scores%d" % h, [P, C], F32) for h in range(HALVES)]
-        pieces = [(0, n * 256, 256) for n in range(4)] + [(1, n * BANK, BANK) for n in range(2)]
+        pieces = [(0, n * 256, 256) for n in range(4)] + [(1, 0, 512), (1, 512, 256), (1, 768, 256)]
         for n, (h, first, width) in enumerate(pieces):
             nc.tensor.matmul_mx(
                 out=banks[n][:, :width],
@@ -99,30 +99,25 @@ def tile_attend_vqattention_pl_kernel(tc, query, book_words, book_scales, size, 
             nc.tensor.transpose(size_bank[:, r * P : (r + 1) * P], size_cols[:, r : r + 1].to_broadcast([P, P]), ident[:])
 
         picked = sbuf("picked", [P, HALVES, I], F32, tag="q_grouped1")
-
-        neg_max = [sbuf("neg_max%d" % h, [P, 1], F32) for h in range(HALVES)]
+        neg_max = sbuf("neg_max", [P, HALVES], F32)
         total = [sbuf("total%d" % h, [P, 1], F32) for h in range(HALVES)]
-        inv_total = [sbuf("inv_total%d" % h, [P, 1], F32) for h in range(HALVES)]
-        gathered = {}
-
-        def gather_values(t, reused):
-            gathered[t] = sbuf("gathered%d" % t, [P, I], BF16, tag=reused)
-            nc.vector.tensor_copy(gathered[t][:], pools[t][:].indirect(token_list[:]))
 
         pool0_bf16 = sbuf("pool0_bf16", [P, T], BF16, tag="size_cols")
-        nc.scalar.activation(pool0_bf16[:], pools[0][:], ACT.Copy)
+        for n in range(2):
+            nc.scalar.activation(pool0_bf16[:, n * T // 2 : (n + 1) * T // 2], pool0_parts[n][:], ACT.Copy)
         for h in range(HALVES):
             nc.vector.tensor_copy(picked[:, h, :], scores[h][:].indirect(code_list[:]))
-        for h, reused in enumerate(["scores1", "scores0"]):
-            negated = sbuf("negated%d" % h, [P, I], BF16, tag=reused)
-            nc.vector.tensor_scalar(negated[:], picked[:, h, :], -1.0, None, ALU.mult, ALU.min, accum_out=neg_max[h][:])
-        probs = sbuf("probs", [P, HALVES, I], F32, tag="pool0")
+        nc.vector.tensor_reduce(neg_max[:], picked[:], AXIS.X, ALU.max, negate=True)
+        probs = sbuf("probs", [P, HALVES, I], F32, tag="pool0_part1")
         for h in range(HALVES):
-            nc.scalar.activation(probs[:, h, :], picked[:, h, :], ACT.Exp, bias=neg_max[h][:], accum_out=total[h][:])
-        gathered[0] = sbuf("gathered0", [P, I], BF16, tag="q_grouped1")
-        nc.scalar.activation(gathered[0][:], pool0_bf16[:].indirect(token_list[:]), ACT.Copy)
-        gather_values(1, "scores0")
-        weights = [sbuf("weights0", [P, I], BF16), sbuf("weights1", [P, I], BF16, tag="pool1")]
+            nc.scalar.activation(probs[:, h, :], picked[:, h, :], ACT.Exp, bias=neg_max[:, h : h + 1], accum_out=total[h][:])
+        first = sbuf("gathered0", [P, I], BF16, tag="q_grouped1")
+        nc.scalar.activation(first[:], pool0_bf16[:].indirect(token_list[:]), ACT.Copy)
+        middle = sbuf("gathered12", [P, 2, I], BF16, tag="pool0_part0")
+        for t in (1, 2):
+            nc.vector.tensor_copy(middle[:, t - 1, :], pools[t][:].indirect(token_list[:]))
+        inv_total = [sbuf("inv_total0", [P, 1], F32, tag="pool2"), sbuf("inv_total1", [P, 1], F32)]
+        weights = [sbuf("weights%d" % h, [P, I], BF16) for h in range(HALVES)]
         for h in range(HALVES):
             nc.vector.reciprocal(inv_total[h][:], total[h][:])
         for h in range(HALVES):
@@ -134,29 +129,28 @@ def tile_attend_vqattention_pl_kernel(tc, query, book_words, book_scales, size, 
                 ALU.mult,
                 ALU.mult,
             )
-        gather_values(2, "inv_total0")
-        gather_values(3, "inv_total1")
+        last = sbuf("gathered3", [P, I], BF16, tag="pool2")
+        nc.vector.tensor_copy(last[:], pools[3][:].indirect(token_list[:]))
+        gathered = [first[:], middle[:, 0, :], middle[:, 1, :], last[:]]
 
         def turn(src, bank, dst):
-            words = src[:].bitcast(F32)
+            words = src.bitcast(F32)
             for u in range(2):
                 nc.tensor.transpose(bank[:, u * P : (u + 1) * P], words[:, u : I // 2 : 2], ident[:])
             nc.scalar.copy(dst.bitcast(F32).rearrange("p (m u) -> p m u", u=2), bank[:, : 2 * P].rearrange("p (u m) -> p m u", u=2))
 
-        early = sbuf("early", [P, 4 * I], BF16, tag="size_cols")
+        grouped = sbuf("grouped", [P, 6 * I], BF16, tag="size_cols")
+        for t, bank in [(1, 2), (2, 0), (0, 3)]:
+            turn(gathered[t], banks[bank], grouped[:, (2 + t) * I : (3 + t) * I])
         for h in range(HALVES):
-            turn(weights[h], banks[1 if h == 0 else 6], early[:, h * I : (h + 1) * I])
-        turn(gathered[1], size_bank, early[:, 3 * I :])
-        turn(gathered[0], banks[3], early[:, 2 * I : 3 * I])
-        late = sbuf("late", [P, 2 * I], BF16)
-        turn(gathered[2], banks[0], late[:, :I])
-        turn(gathered[3], banks[2], late[:, I:])
+            turn(weights[h][:], banks[1 if h == 0 else 6], grouped[:, h * I : (h + 1) * I])
+        turn(gathered[3], banks[2], grouped[:, 5 * I :])
         early_codes = sbuf("early_codes", [P, 4 * P], U32, tag="pool3")
         early_plane = sbuf("early_plane", [P, 4 * P], U8)
-        nc.vector.quantize_mx(out=early_codes[:].bitcast(FP8X4), scales=early_plane[:], in_=early[:])
+        nc.vector.quantize_mx(out=early_codes[:].bitcast(FP8X4), scales=early_plane[:], in_=grouped[:, : 4 * I])
         late_codes = sbuf("late_codes", [P, 2 * P], U32)
         late_plane = sbuf("late_plane", [P, 2 * P], U8)
-        nc.vector.quantize_mx(out=late_codes[:].bitcast(FP8X4), scales=late_plane[:], in_=late[:])
+        nc.vector.quantize_mx(out=late_codes[:].bitcast(FP8X4), scales=late_plane[:], in_=grouped[:, 4 * I :])
 
         out_banks = [banks[5], banks[7]]
         result = sbuf("result", [P, PACK, Q], F32)

@@ -68,10 +68,12 @@ def tile_attend_vqattention_pl_kernel(tc, query, book_words, book_scales, size, 
 
         q_codes, q_planes = [], []
         q_grouped = [sbuf("q_grouped%d" % h, [P, P, PACK], BF16) for h in range(HALVES)]
-        by_query = query_raw[:].rearrange("p j q -> p q j")
-        nc.vector.tensor_copy(q_grouped[0][:, : P // 2, :], by_query[:, : P // 2, :])
-        nc.scalar.copy(q_grouped[0][:, P // 2 :, :], by_query[:, P // 2 : P, :])
-        nc.scalar.copy(q_grouped[1][:], by_query[:, P:, :])
+        for h in range(HALVES):
+            src = query_raw[:, :, h * P : (h + 1) * P].rearrange("p j q -> p q j")
+            if h == 0:
+                nc.vector.tensor_copy(q_grouped[h][:], src)
+            else:
+                nc.scalar.copy(q_grouped[h][:], src)
         for h in range(HALVES):
             codes = sbuf("q_codes%d" % h, [P, P], U32)
             plane = sbuf("q_plane%d" % h, [P, P], U8)
@@ -101,6 +103,7 @@ def tile_attend_vqattention_pl_kernel(tc, query, book_words, book_scales, size, 
         picked = sbuf("picked", [P, HALVES, I], F32, tag="q_grouped1")
         neg_max = sbuf("neg_max", [P, HALVES], F32)
         total = [sbuf("total%d" % h, [P, 1], F32) for h in range(HALVES)]
+        inv_total = [sbuf("inv_total%d" % h, [P, 1], F32) for h in range(HALVES)]
 
         pool0_bf16 = sbuf("pool0_bf16", [P, T], BF16, tag="size_cols")
         for n in range(2):
@@ -113,10 +116,8 @@ def tile_attend_vqattention_pl_kernel(tc, query, book_words, book_scales, size, 
             nc.scalar.activation(probs[:, h, :], picked[:, h, :], ACT.Exp, bias=neg_max[:, h : h + 1], accum_out=total[h][:])
         first = sbuf("gathered0", [P, I], BF16, tag="q_grouped1")
         nc.scalar.activation(first[:], pool0_bf16[:].indirect(token_list[:]), ACT.Copy)
-        middle = sbuf("gathered12", [P, 2, I], BF16, tag="pool0_part0")
-        for t in (1, 2):
-            nc.vector.tensor_copy(middle[:, t - 1, :], pools[t][:].indirect(token_list[:]))
-        inv_total = [sbuf("inv_total0", [P, 1], F32, tag="pool2"), sbuf("inv_total1", [P, 1], F32)]
+        second = sbuf("gathered1", [P, I], BF16, tag="pool0_part0")
+        nc.vector.tensor_copy(second[:], pools[1][:].indirect(token_list[:]))
         weights = [sbuf("weights%d" % h, [P, I], BF16) for h in range(HALVES)]
         for h in range(HALVES):
             nc.vector.reciprocal(inv_total[h][:], total[h][:])
@@ -129,9 +130,11 @@ def tile_attend_vqattention_pl_kernel(tc, query, book_words, book_scales, size, 
                 ALU.mult,
                 ALU.mult,
             )
-        last = sbuf("gathered3", [P, I], BF16, tag="pool2")
+        third = sbuf("gathered2", [P, I], BF16, tag="inv_total0")
+        nc.vector.tensor_copy(third[:], pools[2][:].indirect(token_list[:]))
+        last = sbuf("gathered3", [P, I], BF16, tag="inv_total1")
         nc.vector.tensor_copy(last[:], pools[3][:].indirect(token_list[:]))
-        gathered = [first[:], middle[:, 0, :], middle[:, 1, :], last[:]]
+        gathered = [first[:], second[:], third[:], last[:]]
 
         def turn(src, bank, dst):
             words = src.bitcast(F32)
@@ -140,11 +143,10 @@ def tile_attend_vqattention_pl_kernel(tc, query, book_words, book_scales, size, 
             nc.scalar.copy(dst.bitcast(F32).rearrange("p (m u) -> p m u", u=2), bank[:, : 2 * P].rearrange("p (u m) -> p m u", u=2))
 
         grouped = sbuf("grouped", [P, 6 * I], BF16, tag="size_cols")
-        for t, bank in [(1, 2), (2, 0), (0, 3)]:
-            turn(gathered[t], banks[bank], grouped[:, (2 + t) * I : (3 + t) * I])
         for h in range(HALVES):
             turn(weights[h][:], banks[1 if h == 0 else 6], grouped[:, h * I : (h + 1) * I])
-        turn(gathered[3], banks[2], grouped[:, 5 * I :])
+        for t, bank in [(1, 2), (0, 3), (2, 0), (3, 2)]:
+            turn(gathered[t], banks[bank], grouped[:, (2 + t) * I : (3 + t) * I])
         early_codes = sbuf("early_codes", [P, 4 * P], U32, tag="pool3")
         early_plane = sbuf("early_plane", [P, 4 * P], U8)
         nc.vector.quantize_mx(out=early_codes[:].bitcast(FP8X4), scales=early_plane[:], in_=grouped[:, : 4 * I])

@@ -59,10 +59,6 @@ def tile_attend_vqattention_pl_kernel(tc, query, book_words, book_scales, size, 
         for t in range(1, PACK):
             nc.sync.dma_start(out=pools[t][:], in_=vals_rows[t])
 
-        zero = sbuf("zero", [P, 1], F32)
-        nc.vector.memset(zero[:], 0.0)
-        warm = sbuf("warm", [P, 1], F32)
-        nc.scalar.activation(warm[:], zero[:], ACT.Exp)
         ident = sbuf("ident", [P, P], F32)
         make_identity(nc, ident[:])
 
@@ -73,7 +69,7 @@ def tile_attend_vqattention_pl_kernel(tc, query, book_words, book_scales, size, 
             if h == 0:
                 nc.vector.tensor_copy(q_grouped[h][:], src)
             else:
-                nc.scalar.copy(q_grouped[h][:], src)
+                nc.scalar.activation(q_grouped[h][:], src, ACT.Copy)
         for h in range(HALVES):
             codes = sbuf("q_codes%d" % h, [P, P], U32)
             plane = sbuf("q_plane%d" % h, [P, P], U8)
@@ -81,7 +77,7 @@ def tile_attend_vqattention_pl_kernel(tc, query, book_words, book_scales, size, 
             q_codes.append(codes)
             q_planes.append(plane)
 
-        scores = [sbuf("scores%d" % h, [P, C], F32) for h in range(HALVES)]
+        scores = [sbuf("scores0", [P, C], F32, tag="q_grouped1"), sbuf("scores1", [P, C], F32)]
         pieces = [(0, n * 256, 256) for n in range(4)] + [(1, 0, 512), (1, 512, 256), (1, 768, 256)]
         for n, (h, first, width) in enumerate(pieces):
             nc.tensor.matmul_mx(
@@ -100,7 +96,7 @@ def tile_attend_vqattention_pl_kernel(tc, query, book_words, book_scales, size, 
         for r in range(PACK):
             nc.tensor.transpose(size_bank[:, r * P : (r + 1) * P], size_cols[:, r : r + 1].to_broadcast([P, P]), ident[:])
 
-        picked = sbuf("picked", [P, HALVES, I], F32, tag="q_grouped1")
+        picked = sbuf("picked", [P, HALVES, I], F32)
         neg_max = sbuf("neg_max", [P, HALVES], F32)
         total = [sbuf("total%d" % h, [P, 1], F32) for h in range(HALVES)]
         inv_total = [sbuf("inv_total%d" % h, [P, 1], F32) for h in range(HALVES)]
@@ -114,7 +110,7 @@ def tile_attend_vqattention_pl_kernel(tc, query, book_words, book_scales, size, 
         probs = sbuf("probs", [P, HALVES, I], F32, tag="pool0_part1")
         for h in range(HALVES):
             nc.scalar.activation(probs[:, h, :], picked[:, h, :], ACT.Exp, bias=neg_max[:, h : h + 1], accum_out=total[h][:])
-        first = sbuf("gathered0", [P, I], BF16, tag="q_grouped1")
+        first = sbuf("gathered0", [P, I], BF16, tag="picked")
         nc.scalar.activation(first[:], pool0_bf16[:].indirect(token_list[:]), ACT.Copy)
         second = sbuf("gathered1", [P, I], BF16, tag="pool0_part0")
         nc.vector.tensor_copy(second[:], pools[1][:].indirect(token_list[:]))
@@ -200,7 +196,7 @@ def tile_attend_vqattention_pl_kernel(tc, query, book_words, book_scales, size, 
         nc.scalar.dma_start(out=out_rows[:, 2:, :], in_=result[:, 2:, :])
         nc.sync.dma_start(out=out_1[0].rearrange("p c r -> p (c r)").bitcast(I32), in_=o_codes[:].bitcast(I32))
         for quad in range(4):
-            queue = nc.sync if quad != 3 else nc.scalar
+            queue = nc.sync if quad < 2 else nc.scalar
             queue.dma_start(
                 out=out_2[0, 4 * quad : 4 * quad + 4, :].bitcast(I32),
                 in_=o_plane[32 * quad : 32 * quad + 4, :].bitcast(I32),

@@ -35,23 +35,25 @@ def tile_attend_vqattention_pl_kernel(tc, query, book_words, book_scales, size, 
 
         banks = [ps.tile([P, BANK], F32, name="bank%d" % n) for n in range(8)]
 
-        query_raw = sbuf("query_raw", [P, PACK, Q], F32)
+        query_raw = [sbuf("query_raw%d" % h, [P, PACK, P], F32) for h in range(HALVES)]
         book_plane = sbuf("book_plane", [P, C], U8)
         book_codes = sbuf("book_codes", [P, 2 * C], U8)
-        nc.sync.dma_start(out=query_raw[:], in_=query.rearrange("(p j) q -> p j q", j=PACK))
+        query_rows = query.rearrange("(p j) q -> p j q", j=PACK)
+        nc.sync.dma_start(out=query_raw[0][:], in_=query_rows[:, :, :P])
         nc.sync.dma_start(out=book_codes[:].bitcast(I32), in_=book_words[0].bitcast(I32))
         for quad, queue in enumerate([nc.scalar, nc.scalar, nc.sync, nc.scalar]):
             queue.dma_start(
                 out=book_plane[32 * quad : 32 * quad + 4, :].bitcast(I32),
                 in_=book_scales[0, 4 * quad : 4 * quad + 4, :].bitcast(I32),
             )
+        nc.sync.dma_start(out=query_raw[1][:], in_=query_rows[:, :, P:])
         vals_rows = vals.rearrange("(m t) n -> t m n", t=PACK)
         pool0_parts = [sbuf("pool0_part%d" % n, [P, T // 2], F32) for n in range(2)]
         pools = {t: sbuf("pool%d" % t, [P, T], F32) for t in range(1, PACK)}
-        for n in range(2):
-            nc.sync.dma_start(out=pool0_parts[n][:], in_=vals_rows[0][:, n * T // 2 : (n + 1) * T // 2])
+        nc.sync.dma_start(out=pool0_parts[0][:], in_=vals_rows[0][:, : T // 2])
         code_list = sbuf("code_list", [P, I // 16], U16)
         nc.sync.dma_start(code_list[:], offs)
+        nc.sync.dma_start(out=pool0_parts[1][:], in_=vals_rows[0][:, T // 2 :])
         size_cols = sbuf("size_cols", [P, PACK], F32)
         nc.sync.dma_start(out=size_cols[:], in_=size.rearrange("o (s r) -> (o s) r", r=PACK))
         token_list = sbuf("token_list", [P, I // 16], U16)
@@ -63,22 +65,17 @@ def tile_attend_vqattention_pl_kernel(tc, query, book_words, book_scales, size, 
         make_identity(nc, ident[:])
 
         q_codes, q_planes = [], []
-        q_grouped = [sbuf("q_grouped%d" % h, [P, P, PACK], BF16) for h in range(HALVES)]
+        scores = [sbuf("scores%d" % h, [P, C], F32) for h in range(HALVES)]
+        q_grouped = [sbuf("q_grouped0", [P, P * PACK], BF16)[:], scores[0][:, 640:896].bitcast(BF16)]
         for h in range(HALVES):
-            src = query_raw[:, :, h * P : (h + 1) * P].rearrange("p j q -> p q j")
-            if h == 0:
-                nc.vector.tensor_copy(q_grouped[h][:], src)
-            else:
-                nc.scalar.activation(q_grouped[h][:], src, ACT.Copy)
-        for h in range(HALVES):
+            nc.vector.tensor_copy(q_grouped[h].rearrange("p (q j) -> p q j", j=PACK), query_raw[h][:].rearrange("p j q -> p q j"))
             codes = sbuf("q_codes%d" % h, [P, P], U32)
             plane = sbuf("q_plane%d" % h, [P, P], U8)
-            nc.vector.quantize_mx(out=codes[:].bitcast(FP8X4), scales=plane[:], in_=q_grouped[h][:].rearrange("p q j -> p (q j)"))
+            nc.vector.quantize_mx(out=codes[:].bitcast(FP8X4), scales=plane[:], in_=q_grouped[h])
             q_codes.append(codes)
             q_planes.append(plane)
 
-        scores = [sbuf("scores0", [P, C], F32, tag="q_grouped1"), sbuf("scores1", [P, C], F32)]
-        pieces = [(0, n * 256, 256) for n in range(4)] + [(1, 0, 512), (1, 512, 256), (1, 768, 256)]
+        pieces = [(0, 0, 256), (0, 256, 256), (0, 512, 256), (0, 768, 128), (0, 896, 128), (1, 0, 512), (1, 512, 512)]
         for n, (h, first, width) in enumerate(pieces):
             nc.tensor.matmul_mx(
                 out=banks[n][:, :width],
@@ -89,48 +86,50 @@ def tile_attend_vqattention_pl_kernel(tc, query, book_words, book_scales, size, 
                 start=True,
                 stop=True,
             )
-        size_bank = banks[4]
+        size_bank = banks[7]
         for n, (h, first, width) in enumerate(pieces):
-            copy = nc.vector.tensor_copy if h == 0 and n % 2 == 1 else nc.scalar.copy
-            copy(scores[h][:, first : first + width], banks[n][:, :width])
+            if n in (2, 3):
+                nc.vector.tensor_copy(scores[h][:, first : first + width], banks[n][:, :width])
+            else:
+                nc.scalar.activation(scores[h][:, first : first + width], banks[n][:, :width], ACT.Copy)
         for r in range(PACK):
             nc.tensor.transpose(size_bank[:, r * P : (r + 1) * P], size_cols[:, r : r + 1].to_broadcast([P, P]), ident[:])
-
-        picked = sbuf("picked", [P, HALVES, I], F32)
-        neg_max = sbuf("neg_max", [P, HALVES], F32)
-        total = [sbuf("total%d" % h, [P, 1], F32) for h in range(HALVES)]
-        inv_total = [sbuf("inv_total%d" % h, [P, 1], F32) for h in range(HALVES)]
-
-        pool0_bf16 = sbuf("pool0_bf16", [P, T], BF16, tag="size_cols")
+        pool0_bf16 = sbuf("pool0_bf16", [P, T], BF16, tag="q_codes1")
         for n in range(2):
             nc.scalar.activation(pool0_bf16[:, n * T // 2 : (n + 1) * T // 2], pool0_parts[n][:], ACT.Copy)
+
+        picked = [sbuf("picked%d" % h, [P, I], F32) for h in range(HALVES)]
+        neg_max = [sbuf("neg_max0", [P, 1], F32, tag="size_cols"), sbuf("neg_max1", [P, 1], F32)]
+        total = sbuf("total", [P, HALVES], F32)
+
         for h in range(HALVES):
-            nc.vector.tensor_copy(picked[:, h, :], scores[h][:].indirect(code_list[:]))
-        nc.vector.tensor_reduce(neg_max[:], picked[:], AXIS.X, ALU.max, negate=True)
+            nc.vector.tensor_copy(picked[h][:], scores[h][:].indirect(code_list[:]))
+        for h in range(HALVES):
+            nc.vector.tensor_reduce(neg_max[h][:], picked[h][:], AXIS.X, ALU.max, negate=True)
         probs = sbuf("probs", [P, HALVES, I], F32, tag="pool0_part1")
         for h in range(HALVES):
-            nc.scalar.activation(probs[:, h, :], picked[:, h, :], ACT.Exp, bias=neg_max[:, h : h + 1], accum_out=total[h][:])
-        first = sbuf("gathered0", [P, I], BF16, tag="picked")
+            nc.scalar.activation(probs[:, h, :], picked[h][:], ACT.Exp, bias=neg_max[h][:], accum_out=total[:, h : h + 1])
+        first = sbuf("gathered0", [P, I], BF16, tag="picked0")
         nc.scalar.activation(first[:], pool0_bf16[:].indirect(token_list[:]), ACT.Copy)
-        second = sbuf("gathered1", [P, I], BF16, tag="pool0_part0")
+        second = sbuf("gathered1", [P, I], BF16, tag="scores1")
         nc.vector.tensor_copy(second[:], pools[1][:].indirect(token_list[:]))
         weights = [sbuf("weights%d" % h, [P, I], BF16) for h in range(HALVES)]
-        for h in range(HALVES):
-            nc.vector.reciprocal(inv_total[h][:], total[h][:])
+        after_pool1 = sbuf("after_pool1", [P, I // 2 + HALVES], F32, tag="pool1")
+        inv_total = after_pool1[:, I // 2 :]
+        third = after_pool1[:, : I // 2].bitcast(BF16)
+        nc.vector.reciprocal(inv_total, total[:])
+        nc.vector.tensor_copy(third, pools[2][:].indirect(token_list[:]))
         for h in range(HALVES):
             nc.vector.scalar_tensor_tensor(
                 weights[h][:].rearrange("p (s r) -> p s r", r=PACK),
                 probs[:, h, :].rearrange("p (s r) -> p s r", r=PACK),
-                inv_total[h][:],
+                inv_total[:, h : h + 1],
                 size_bank[:].rearrange("p (r s) -> p s r", r=PACK),
                 ALU.mult,
                 ALU.mult,
             )
-        third = sbuf("gathered2", [P, I], BF16, tag="inv_total0")
-        nc.vector.tensor_copy(third[:], pools[2][:].indirect(token_list[:]))
-        last = sbuf("gathered3", [P, I], BF16, tag="inv_total1")
+        last = sbuf("gathered3", [P, I], BF16, tag="total")
         nc.vector.tensor_copy(last[:], pools[3][:].indirect(token_list[:]))
-        gathered = [first[:], second[:], third[:], last[:]]
 
         def turn(src, bank, dst):
             words = src.bitcast(F32)
@@ -138,62 +137,69 @@ def tile_attend_vqattention_pl_kernel(tc, query, book_words, book_scales, size, 
                 nc.tensor.transpose(bank[:, u * P : (u + 1) * P], words[:, u : I // 2 : 2], ident[:])
             nc.scalar.copy(dst.bitcast(F32).rearrange("p (m u) -> p m u", u=2), bank[:, : 2 * P].rearrange("p (u m) -> p m u", u=2))
 
-        grouped = sbuf("grouped", [P, 6 * I], BF16, tag="size_cols")
-        for h in range(HALVES):
-            turn(weights[h][:], banks[1 if h == 0 else 6], grouped[:, h * I : (h + 1) * I])
-        for t, bank in [(1, 2), (0, 3), (2, 0), (3, 2)]:
-            turn(gathered[t], banks[bank], grouped[:, (2 + t) * I : (3 + t) * I])
-        early_codes = sbuf("early_codes", [P, 4 * P], U32, tag="pool3")
-        early_plane = sbuf("early_plane", [P, 4 * P], U8)
-        nc.vector.quantize_mx(out=early_codes[:].bitcast(FP8X4), scales=early_plane[:], in_=grouped[:, : 4 * I])
-        late_codes = sbuf("late_codes", [P, 2 * P], U32)
-        late_plane = sbuf("late_plane", [P, 2 * P], U8)
-        nc.vector.quantize_mx(out=late_codes[:].bitcast(FP8X4), scales=late_plane[:], in_=grouped[:, 4 * I :])
+        grouped = sbuf("grouped", [P, 6 * I], BF16)
+        turn(second[:], banks[0], grouped[:, 3 * I : 4 * I])
+        turn(first[:], banks[1], grouped[:, 2 * I : 3 * I])
+        turn(third, banks[2], grouped[:, 4 * I : 5 * I])
+        turn(weights[0][:], banks[3], grouped[:, :I])
+        turn(weights[1][:], banks[0], grouped[:, I : 2 * I])
+        turn(last[:], banks[1], grouped[:, 5 * I :])
+        codes = sbuf("codes", [P, 6 * P], U32, tag="pool3")
+        planes = sbuf("planes", [P, 6 * P], U8)
+        for first_col, cols in [(0, 4 * P), (4 * P, P), (5 * P, P)]:
+            nc.vector.quantize_mx(
+                out=codes[:, first_col : first_col + cols].bitcast(FP8X4),
+                scales=planes[:, first_col : first_col + cols],
+                in_=grouped[:, PACK * first_col : PACK * (first_col + cols)],
+            )
 
-        out_banks = [banks[5], banks[7]]
-        result = sbuf("result", [P, PACK, Q], F32)
+        out_banks = [[banks[5], banks[6]], [banks[4], banks[2]]]
+        result = [sbuf("result%d" % pair, [P, 2, Q], F32) for pair in range(2)]
         out_rows = out_0.rearrange("(m t) q -> m t q", t=PACK)
+        o_grouped = [sbuf("o_grouped%d" % h, [P, P, PACK], BF16) for h in range(HALVES)]
+        copies = [nc.vector.tensor_copy, nc.scalar.copy]
 
-        def multiply(first, codes, plane):
-            for h in range(HALVES):
-                for n in range(2):
+        def multiply(pair):
+            for n in range(2):
+                t = 2 * pair + n
+                for h in (1, 0):
                     nc.tensor.matmul_mx(
-                        out=out_banks[h][:, (first + n) * P : (first + n + 1) * P],
-                        lhsT=codes[:, n * P : (n + 1) * P].bitcast(FP8X4),
-                        lhsT_scale=plane[:, n * P : (n + 1) * P],
-                        rhs=early_codes[:, h * P : (h + 1) * P].bitcast(FP8X4),
-                        rhs_scale=early_plane[:, h * P : (h + 1) * P],
+                        out=out_banks[pair][h][:, n * P : (n + 1) * P],
+                        lhsT=codes[:, (2 + t) * P : (3 + t) * P].bitcast(FP8X4),
+                        lhsT_scale=planes[:, (2 + t) * P : (3 + t) * P],
+                        rhs=codes[:, h * P : (h + 1) * P].bitcast(FP8X4),
+                        rhs_scale=planes[:, h * P : (h + 1) * P],
                         start=True,
                         stop=True,
                     )
 
-        def copy_out(first, h, copy):
-            copy(
-                result[:, first : first + 2, h * P : (h + 1) * P],
-                out_banks[h][:, first * P : (first + 2) * P].rearrange("p (t q) -> p t q", t=2),
-            )
+        def copy_out(pair, h, copy):
+            copy(result[pair][:, :, h * P : (h + 1) * P], out_banks[pair][h][:, : 2 * P].rearrange("p (t q) -> p t q", t=2))
 
-        multiply(0, early_codes[:, 2 * P :], early_plane[:, 2 * P :])
-        copy_out(0, 0, nc.scalar.copy)
-        copy_out(0, 1, nc.scalar.copy)
-        nc.sync.dma_start(out=out_rows[:, :2, :], in_=result[:, :2, :])
-        multiply(2, late_codes[:], late_plane[:])
+        def group(pair, h):
+            copies[h](o_grouped[h][:, :, 2 * pair : 2 * pair + 2], out_banks[pair][h][:, : 2 * P].rearrange("p (t q) -> p q t", t=2))
 
-        o_grouped = [sbuf("o_grouped%d" % h, [P, P, PACK], BF16) for h in range(HALVES)]
+        multiply(0)
+        for h in range(HALVES):
+            copy_out(0, h, copies[h])
+        nc.sync.dma_start(out=out_rows[:, :2, :], in_=result[0][:])
+        for h in range(HALVES):
+            group(0, h)
+        multiply(1)
+        for h in range(HALVES):
+            group(1, h)
+        for h in range(HALVES):
+            copy_out(1, h, copies[h])
+
         o_codes = sbuf("o_codes", [P, Q], U32)
         o_plane = sbuf("o_plane", [P, Q], U8)
-        for h in range(HALVES):
-            copy = nc.vector.tensor_copy if h == 0 else nc.scalar.copy
-            copy(o_grouped[h][:], out_banks[h][:].rearrange("p (t q) -> p q t", t=PACK))
-        for h in range(HALVES):
+        for h in (1, 0):
             nc.vector.quantize_mx(
                 out=o_codes[:, h * P : (h + 1) * P].bitcast(FP8X4),
                 scales=o_plane[:, h * P : (h + 1) * P],
                 in_=o_grouped[h][:].rearrange("p q t -> p (q t)"),
             )
-        for h in range(HALVES):
-            copy_out(2, h, nc.scalar.copy)
-        nc.scalar.dma_start(out=out_rows[:, 2:, :], in_=result[:, 2:, :])
+        nc.scalar.dma_start(out=out_rows[:, 2:, :], in_=result[1][:])
         nc.sync.dma_start(out=out_1[0].rearrange("p c r -> p (c r)").bitcast(I32), in_=o_codes[:].bitcast(I32))
         for quad in range(4):
             queue = nc.sync if quad < 2 else nc.scalar

@@ -98,6 +98,9 @@ def tile_attend_vqattention_pl_kernel(tc, query, book_words, book_scales, size, 
         for n in range(2):
             nc.scalar.activation(pool0_bf16[:, n * T // 2 : (n + 1) * T // 2], pool0_parts[n][:], ACT.Copy)
 
+        size_row = sbuf("size_row", [P, I], F32, tag="pool0_part0")
+        nc.scalar.activation(size_row[:].rearrange("p (s r) -> p s r", r=PACK), size_bank[:].rearrange("p (r s) -> p s r", r=PACK), ACT.Copy)
+
         picked = [sbuf("picked%d" % h, [P, I], F32) for h in range(HALVES)]
         neg_max = [sbuf("neg_max0", [P, 1], F32, tag="size_cols"), sbuf("neg_max1", [P, 1], F32)]
         total = sbuf("total", [P, HALVES], F32)
@@ -119,15 +122,17 @@ def tile_attend_vqattention_pl_kernel(tc, query, book_words, book_scales, size, 
         third = after_pool1[:, : I // 2].bitcast(BF16)
         nc.vector.reciprocal(inv_total, total[:])
         nc.vector.tensor_copy(third, pools[2][:].indirect(token_list[:]))
-        for h in range(HALVES):
-            nc.vector.scalar_tensor_tensor(
-                weights[h][:].rearrange("p (s r) -> p s r", r=PACK),
-                probs[:, h, :].rearrange("p (s r) -> p s r", r=PACK),
-                inv_total[:, h : h + 1],
-                size_bank[:].rearrange("p (r s) -> p s r", r=PACK),
-                ALU.mult,
-                ALU.mult,
-            )
+        sized = sbuf("sized", [P, I], F32)
+        nc.gpsimd.tensor_tensor(sized[:], probs[:, 0, :], size_row[:], ALU.mult)
+        nc.gpsimd.tensor_scalar(weights[0][:], sized[:], inv_total[:, 0:1], 0.0, ALU.mult, ALU.add)
+        nc.vector.scalar_tensor_tensor(
+            weights[1][:].rearrange("p (s r) -> p s r", r=PACK),
+            probs[:, 1, :].rearrange("p (s r) -> p s r", r=PACK),
+            inv_total[:, 1:2],
+            size_bank[:].rearrange("p (r s) -> p s r", r=PACK),
+            ALU.mult,
+            ALU.mult,
+        )
         last = sbuf("gathered3", [P, I], BF16, tag="total")
         nc.vector.tensor_copy(last[:], pools[3][:].indirect(token_list[:]))
 

@@ -35,25 +35,21 @@ def tile_attend_vqattention_pl_kernel(tc, query, book_words, book_scales, size, 
 
         banks = [ps.tile([P, BANK], F32, name="bank%d" % n) for n in range(8)]
 
-        query_raw = [sbuf("query_raw%d" % h, [P, PACK, P], F32) for h in range(HALVES)]
+        query_raw = sbuf("query_raw", [P, PACK, Q], F32)
         book_plane = sbuf("book_plane", [P, C], U8)
         book_codes = sbuf("book_codes", [P, 2 * C], U8)
-        query_rows = query.rearrange("(p j) q -> p j q", j=PACK)
-        nc.sync.dma_start(out=query_raw[0][:], in_=query_rows[:, :, :P])
+        nc.sync.dma_start(out=query_raw[:], in_=query.rearrange("(p j) q -> p j q", j=PACK))
         nc.sync.dma_start(out=book_codes[:].bitcast(I32), in_=book_words[0].bitcast(I32))
         for quad, queue in enumerate([nc.scalar, nc.scalar, nc.sync, nc.scalar]):
             queue.dma_start(
                 out=book_plane[32 * quad : 32 * quad + 4, :].bitcast(I32),
                 in_=book_scales[0, 4 * quad : 4 * quad + 4, :].bitcast(I32),
             )
-        nc.sync.dma_start(out=query_raw[1][:], in_=query_rows[:, :, P:])
         vals_rows = vals.rearrange("(m t) n -> t m n", t=PACK)
-        pool0_parts = [sbuf("pool0_part%d" % n, [P, T // 2], F32) for n in range(2)]
-        pools = {t: sbuf("pool%d" % t, [P, T], F32) for t in range(1, PACK)}
-        nc.sync.dma_start(out=pool0_parts[0][:], in_=vals_rows[0][:, : T // 2])
+        pools = [sbuf("pool%d" % t, [P, T], F32) for t in range(PACK)]
         code_list = sbuf("code_list", [P, I // 16], U16)
         nc.sync.dma_start(code_list[:], offs)
-        nc.sync.dma_start(out=pool0_parts[1][:], in_=vals_rows[0][:, T // 2 :])
+        nc.sync.dma_start(out=pools[0][:], in_=vals_rows[0])
         size_cols = sbuf("size_cols", [P, PACK], F32)
         nc.sync.dma_start(out=size_cols[:], in_=size.rearrange("o (s r) -> (o s) r", r=PACK))
         token_list = sbuf("token_list", [P, I // 16], U16)
@@ -68,7 +64,12 @@ def tile_attend_vqattention_pl_kernel(tc, query, book_words, book_scales, size, 
         scores = [sbuf("scores%d" % h, [P, C], F32) for h in range(HALVES)]
         q_grouped = [sbuf("q_grouped0", [P, P * PACK], BF16)[:], scores[0][:, 640:896].bitcast(BF16)]
         for h in range(HALVES):
-            nc.vector.tensor_copy(q_grouped[h].rearrange("p (q j) -> p q j", j=PACK), query_raw[h][:].rearrange("p j q -> p q j"))
+            dst = q_grouped[h].rearrange("p (q j) -> p q j", j=PACK)
+            src = query_raw[:, :, h * P : (h + 1) * P].rearrange("p j q -> p q j")
+            if h == 0:
+                nc.vector.tensor_copy(dst, src)
+            else:
+                nc.scalar.activation(dst, src, ACT.Copy)
             codes = sbuf("q_codes%d" % h, [P, P], U32)
             plane = sbuf("q_plane%d" % h, [P, P], U8)
             nc.vector.quantize_mx(out=codes[:].bitcast(FP8X4), scales=plane[:], in_=q_grouped[h])
@@ -95,11 +96,10 @@ def tile_attend_vqattention_pl_kernel(tc, query, book_words, book_scales, size, 
         for r in range(PACK):
             nc.tensor.transpose(size_bank[:, r * P : (r + 1) * P], size_cols[:, r : r + 1].to_broadcast([P, P]), ident[:])
         pool0_bf16 = sbuf("pool0_bf16", [P, T], BF16, tag="q_codes1")
-        for n in range(2):
-            nc.scalar.activation(pool0_bf16[:, n * T // 2 : (n + 1) * T // 2], pool0_parts[n][:], ACT.Copy)
-
-        size_row = sbuf("size_row", [P, I], F32, tag="pool0_part0")
-        nc.scalar.activation(size_row[:].rearrange("p (s r) -> p s r", r=PACK), size_bank[:].rearrange("p (r s) -> p s r", r=PACK), ACT.Copy)
+        nc.scalar.activation(pool0_bf16[:], pools[0][:], ACT.Copy)
+        after_pool0 = sbuf("after_pool0", [P, 3, I], F32, tag="pool0")
+        size_row = after_pool0[:, 2, :]
+        nc.scalar.activation(size_row.rearrange("p (s r) -> p s r", r=PACK), size_bank[:].rearrange("p (r s) -> p s r", r=PACK), ACT.Copy)
 
         picked = [sbuf("picked%d" % h, [P, I], F32) for h in range(HALVES)]
         neg_max = [sbuf("neg_max0", [P, 1], F32, tag="size_cols"), sbuf("neg_max1", [P, 1], F32)]
@@ -109,7 +109,7 @@ def tile_attend_vqattention_pl_kernel(tc, query, book_words, book_scales, size, 
             nc.vector.tensor_copy(picked[h][:], scores[h][:].indirect(code_list[:]))
         for h in range(HALVES):
             nc.vector.tensor_reduce(neg_max[h][:], picked[h][:], AXIS.X, ALU.max, negate=True)
-        probs = sbuf("probs", [P, HALVES, I], F32, tag="pool0_part1")
+        probs = after_pool0
         for h in range(HALVES):
             nc.scalar.activation(probs[:, h, :], picked[h][:], ACT.Exp, bias=neg_max[h][:], accum_out=total[:, h : h + 1])
         first = sbuf("gathered0", [P, I], BF16, tag="picked0")
@@ -123,7 +123,7 @@ def tile_attend_vqattention_pl_kernel(tc, query, book_words, book_scales, size, 
         nc.vector.reciprocal(inv_total, total[:])
         nc.vector.tensor_copy(third, pools[2][:].indirect(token_list[:]))
         sized = sbuf("sized", [P, I], F32)
-        nc.gpsimd.tensor_tensor(sized[:], probs[:, 0, :], size_row[:], ALU.mult)
+        nc.gpsimd.tensor_tensor(sized[:], probs[:, 0, :], size_row, ALU.mult)
         nc.gpsimd.tensor_scalar(weights[0][:], sized[:], inv_total[:, 0:1], 0.0, ALU.mult, ALU.add)
         nc.vector.scalar_tensor_tensor(
             weights[1][:].rearrange("p (s r) -> p s r", r=PACK),

@@ -46,14 +46,16 @@ def tile_attend_vqattention_pl_kernel(tc, query, book_words, book_scales, size, 
                 in_=book_scales[0, 4 * quad : 4 * quad + 4, :].bitcast(I32),
             )
         vals_rows = vals.rearrange("(m t) n -> t m n", t=PACK)
-        pools = [sbuf("pool%d" % t, [P, T], F32) for t in range(PACK)]
+        pool0_parts = [sbuf("pool0_part%d" % n, [P, T // 2], F32) for n in range(2)]
+        pools = {t: sbuf("pool%d" % t, [P, T], F32) for t in range(1, PACK)}
         code_list = sbuf("code_list", [P, I // 16], U16)
         nc.sync.dma_start(code_list[:], offs)
-        nc.sync.dma_start(out=pools[0][:], in_=vals_rows[0])
+        nc.sync.dma_start(out=pool0_parts[0][:], in_=vals_rows[0][:, : T // 2])
         size_cols = sbuf("size_cols", [P, PACK], F32)
         nc.sync.dma_start(out=size_cols[:], in_=size.rearrange("o (s r) -> (o s) r", r=PACK))
         token_list = sbuf("token_list", [P, I // 16], U16)
         nc.sync.dma_start(token_list[:], offs2)
+        nc.sync.dma_start(out=pool0_parts[1][:], in_=vals_rows[0][:, T // 2 :])
         for t in range(1, PACK):
             nc.sync.dma_start(out=pools[t][:], in_=vals_rows[t])
 
@@ -61,8 +63,7 @@ def tile_attend_vqattention_pl_kernel(tc, query, book_words, book_scales, size, 
         make_identity(nc, ident[:])
 
         q_codes, q_planes = [], []
-        scores = [sbuf("scores%d" % h, [P, C], F32) for h in range(HALVES)]
-        q_grouped = [sbuf("q_grouped0", [P, P * PACK], BF16)[:], scores[0][:, 640:896].bitcast(BF16)]
+        q_grouped = [sbuf("q_grouped%d" % h, [P, P * PACK], BF16)[:] for h in range(HALVES)]
         for h in range(HALVES):
             dst = q_grouped[h].rearrange("p (q j) -> p q j", j=PACK)
             src = query_raw[:, :, h * P : (h + 1) * P].rearrange("p j q -> p q j")
@@ -76,7 +77,7 @@ def tile_attend_vqattention_pl_kernel(tc, query, book_words, book_scales, size, 
             q_codes.append(codes)
             q_planes.append(plane)
 
-        pieces = [(0, 0, 256), (0, 256, 256), (0, 512, 256), (0, 768, 128), (0, 896, 128), (1, 0, 512), (1, 512, 512)]
+        pieces = [(0, n * 256, 256) for n in range(4)] + [(1, 0, 512), (1, 512, 256), (1, 768, 256)]
         for n, (h, first, width) in enumerate(pieces):
             nc.tensor.matmul_mx(
                 out=banks[n][:, :width],
@@ -88,48 +89,51 @@ def tile_attend_vqattention_pl_kernel(tc, query, book_words, book_scales, size, 
                 stop=True,
             )
         size_bank = banks[7]
+        pool0_bf16 = sbuf("pool0_bf16", [P, T], BF16, tag="q_grouped1")
+        nc.vector.tensor_copy(pool0_bf16[:, : T // 2], pool0_parts[0][:])
+        scores = [sbuf("scores%d" % h, [P, C], F32) for h in range(HALVES)]
         for n, (h, first, width) in enumerate(pieces):
-            if n in (2, 3):
-                nc.vector.tensor_copy(scores[h][:, first : first + width], banks[n][:, :width])
-            else:
-                nc.scalar.activation(scores[h][:, first : first + width], banks[n][:, :width], ACT.Copy)
+            nc.scalar.copy(scores[h][:, first : first + width], banks[n][:, :width])
         for r in range(PACK):
             nc.tensor.transpose(size_bank[:, r * P : (r + 1) * P], size_cols[:, r : r + 1].to_broadcast([P, P]), ident[:])
-        pool0_bf16 = sbuf("pool0_bf16", [P, T], BF16, tag="q_codes1")
-        nc.scalar.activation(pool0_bf16[:], pools[0][:], ACT.Copy)
-        after_pool0 = sbuf("after_pool0", [P, 3, I], F32, tag="pool0")
-        size_row = after_pool0[:, 2, :]
+        cast_late = pool0_bf16[:, T // 2 :]
+        nc.scalar.activation(cast_late, pool0_parts[1][:], ACT.Copy)
+        after_pool0 = sbuf("after_pool0", [P, 3 * I], F32, tag="pool0_part1")
+        size_row = after_pool0[:, :I]
         nc.scalar.activation(size_row.rearrange("p (s r) -> p s r", r=PACK), size_bank[:].rearrange("p (r s) -> p s r", r=PACK), ACT.Copy)
 
-        picked = [sbuf("picked%d" % h, [P, I], F32) for h in range(HALVES)]
-        neg_max = [sbuf("neg_max0", [P, 1], F32, tag="size_cols"), sbuf("neg_max1", [P, 1], F32)]
+        picked = [sbuf("picked0", [P, I], F32, tag="pool0_part0"), sbuf("picked1", [P, I], F32)]
+        neg_max = [sbuf("neg_max0", [P, 1], F32), sbuf("neg_max1", [P, 1], F32, tag="size_cols")]
         total = sbuf("total", [P, HALVES], F32)
 
         for h in range(HALVES):
             nc.vector.tensor_copy(picked[h][:], scores[h][:].indirect(code_list[:]))
         for h in range(HALVES):
             nc.vector.tensor_reduce(neg_max[h][:], picked[h][:], AXIS.X, ALU.max, negate=True)
-        probs = after_pool0
+        probs = [after_pool0[:, (1 + h) * I : (2 + h) * I] for h in range(HALVES)]
         for h in range(HALVES):
-            nc.scalar.activation(probs[:, h, :], picked[h][:], ACT.Exp, bias=neg_max[h][:], accum_out=total[:, h : h + 1])
-        first = sbuf("gathered0", [P, I], BF16, tag="picked0")
+            nc.scalar.activation(probs[h], picked[h][:], ACT.Exp, bias=neg_max[h][:], accum_out=total[:, h : h + 1])
+        first = sbuf("gathered0", [P, I], BF16, tag="pool0_part0")
         nc.scalar.activation(first[:], pool0_bf16[:].indirect(token_list[:]), ACT.Copy)
         second = sbuf("gathered1", [P, I], BF16, tag="scores1")
         nc.vector.tensor_copy(second[:], pools[1][:].indirect(token_list[:]))
         weights = [sbuf("weights%d" % h, [P, I], BF16) for h in range(HALVES)]
-        after_pool1 = sbuf("after_pool1", [P, I // 2 + HALVES], F32, tag="pool1")
-        inv_total = after_pool1[:, I // 2 :]
-        third = after_pool1[:, : I // 2].bitcast(BF16)
-        nc.vector.reciprocal(inv_total, total[:])
+        inv_total = sbuf("inv_total", [P, HALVES], F32)
+        third = sbuf("gathered2", [P, I], BF16, tag="picked1")[:]
+        nc.vector.reciprocal(inv_total[:], total[:])
         nc.vector.tensor_copy(third, pools[2][:].indirect(token_list[:]))
-        sized = sbuf("sized", [P, I], F32)
-        nc.gpsimd.tensor_tensor(sized[:], probs[:, 0, :], size_row, ALU.mult)
-        nc.gpsimd.tensor_scalar(weights[0][:], sized[:], inv_total[:, 0:1], 0.0, ALU.mult, ALU.add)
+        split = 256
+        shares = [(0, I), (1, split)]
+        sized = [sbuf("sized%d" % h, [P, cols], F32) for h, cols in shares]
+        for h, cols in shares:
+            nc.gpsimd.tensor_tensor(sized[h][:], probs[h][:, :cols], size_row[:, :cols], ALU.mult)
+        for h, cols in shares:
+            nc.gpsimd.tensor_scalar(weights[h][:, :cols], sized[h][:], inv_total[:, h : h + 1], 0.0, ALU.mult, ALU.add)
         nc.vector.scalar_tensor_tensor(
-            weights[1][:].rearrange("p (s r) -> p s r", r=PACK),
-            probs[:, 1, :].rearrange("p (s r) -> p s r", r=PACK),
+            weights[1][:, split:].rearrange("p (s r) -> p s r", r=PACK),
+            probs[1][:, split:].rearrange("p (s r) -> p s r", r=PACK),
             inv_total[:, 1:2],
-            size_bank[:].rearrange("p (r s) -> p s r", r=PACK),
+            size_bank[:].rearrange("p (r s) -> p s r", r=PACK)[:, split // PACK :, :],
             ALU.mult,
             ALU.mult,
         )

@@ -48,15 +48,16 @@ def tile_attend_vqattention_pl_kernel(tc, query, book_words, book_scales, size, 
         vals_rows = vals.rearrange("(m t) n -> t m n", t=PACK)
         pool0_parts = [sbuf("pool0_part%d" % n, [P, T // 2], F32) for n in range(2)]
         pools = {t: sbuf("pool%d" % t, [P, T], F32) for t in range(1, PACK)}
-        code_list = sbuf("code_list", [P, I // 16], U16)
-        nc.sync.dma_start(code_list[:], offs)
-        nc.sync.dma_start(out=pool0_parts[0][:], in_=vals_rows[0][:, : T // 2])
         size_cols = sbuf("size_cols", [P, PACK], F32)
         nc.sync.dma_start(out=size_cols[:], in_=size.rearrange("o (s r) -> (o s) r", r=PACK))
+        nc.sync.dma_start(out=pool0_parts[0][:], in_=vals_rows[0][:, : T // 2])
+        code_list = sbuf("code_list", [P, I // 16], U16)
+        nc.sync.dma_start(code_list[:], offs)
+        nc.sync.dma_start(out=pools[1][:], in_=vals_rows[1])
         token_list = sbuf("token_list", [P, I // 16], U16)
         nc.sync.dma_start(token_list[:], offs2)
         nc.sync.dma_start(out=pool0_parts[1][:], in_=vals_rows[0][:, T // 2 :])
-        for t in range(1, PACK):
+        for t in range(2, PACK):
             nc.sync.dma_start(out=pools[t][:], in_=vals_rows[t])
 
         ident = sbuf("ident", [P, P], F32)
@@ -96,48 +97,40 @@ def tile_attend_vqattention_pl_kernel(tc, query, book_words, book_scales, size, 
             nc.scalar.copy(scores[h][:, first : first + width], banks[n][:, :width])
         for r in range(PACK):
             nc.tensor.transpose(size_bank[:, r * P : (r + 1) * P], size_cols[:, r : r + 1].to_broadcast([P, P]), ident[:])
-        cast_late = pool0_bf16[:, T // 2 :]
-        nc.scalar.activation(cast_late, pool0_parts[1][:], ACT.Copy)
-        after_pool0 = sbuf("after_pool0", [P, 3 * I], F32, tag="pool0_part1")
-        size_row = after_pool0[:, :I]
+        size_row = sbuf("size_row", [P, I], F32)[:]
         nc.scalar.activation(size_row.rearrange("p (s r) -> p s r", r=PACK), size_bank[:].rearrange("p (r s) -> p s r", r=PACK), ACT.Copy)
 
-        picked = [sbuf("picked0", [P, I], F32, tag="pool0_part0"), sbuf("picked1", [P, I], F32)]
-        neg_max = [sbuf("neg_max0", [P, 1], F32), sbuf("neg_max1", [P, 1], F32, tag="size_cols")]
-        total = sbuf("total", [P, HALVES], F32)
-
-        for h in range(HALVES):
-            nc.vector.tensor_copy(picked[h][:], scores[h][:].indirect(code_list[:]))
-        for h in range(HALVES):
-            nc.vector.tensor_reduce(neg_max[h][:], picked[h][:], AXIS.X, ALU.max, negate=True)
-        probs = [after_pool0[:, (1 + h) * I : (2 + h) * I] for h in range(HALVES)]
-        for h in range(HALVES):
-            nc.scalar.activation(probs[h], picked[h][:], ACT.Exp, bias=neg_max[h][:], accum_out=total[:, h : h + 1])
-        first = sbuf("gathered0", [P, I], BF16, tag="pool0_part0")
+        after_size = sbuf("after_size", [P, I + 1], F32, tag="size_cols")
+        picked = [sbuf("picked0", [P, I], F32, tag="pool0_part0")[:], after_size[:, :I]]
+        total = [sbuf("total%d" % h, [P, 1], F32) for h in range(HALVES)]
+        inv_total = [sbuf("inv_total%d" % h, [P, 1], F32) for h in range(HALVES)]
+        neg_max0 = after_size[:, I:]
+        nc.vector.tensor_copy(picked[0], scores[0][:].indirect(code_list[:]))
+        nc.vector.tensor_reduce(neg_max0, picked[0], AXIS.X, ALU.max, negate=True)
+        nc.vector.tensor_copy(picked[1], scores[1][:].indirect(code_list[:]))
+        probs = [sbuf("probs0", [P, I], F32)[:]]
+        nc.scalar.activation(probs[0], picked[0], ACT.Exp, bias=neg_max0, accum_out=total[0][:])
+        nc.vector.reciprocal(inv_total[0][:], total[0][:])
+        after_exp0 = sbuf("after_exp0", [P, I // 2 + 1], F32, tag="pool0_part0")
+        neg_max1 = after_exp0[:, I // 2 :]
+        second = after_exp0[:, : I // 2].bitcast(BF16)
+        nc.vector.tensor_reduce(neg_max1, picked[1], AXIS.X, ALU.max, negate=True)
+        nc.scalar.activation(pool0_bf16[:, T // 2 :], pool0_parts[1][:], ACT.Copy)
+        after_cast = sbuf("after_cast", [P, 4 * I], F32, tag="pool0_part1")
+        probs.append(after_cast[:, :I])
+        nc.scalar.activation(probs[1], picked[1], ACT.Exp, bias=neg_max1, accum_out=total[1][:])
+        first = sbuf("gathered0", [P, I], BF16)
         nc.scalar.activation(first[:], pool0_bf16[:].indirect(token_list[:]), ACT.Copy)
-        second = sbuf("gathered1", [P, I], BF16, tag="scores1")
-        nc.vector.tensor_copy(second[:], pools[1][:].indirect(token_list[:]))
-        weights = [sbuf("weights%d" % h, [P, I], BF16) for h in range(HALVES)]
-        inv_total = sbuf("inv_total", [P, HALVES], F32)
-        third = sbuf("gathered2", [P, I], BF16, tag="picked1")[:]
-        nc.vector.reciprocal(inv_total[:], total[:])
+        nc.vector.tensor_copy(second, pools[1][:].indirect(token_list[:]))
+        nc.vector.reciprocal(inv_total[1][:], total[1][:])
+        third = sbuf("gathered2", [P, I], BF16)[:]
         nc.vector.tensor_copy(third, pools[2][:].indirect(token_list[:]))
-        split = 256
-        shares = [(0, I), (1, split)]
-        sized = [sbuf("sized%d" % h, [P, cols], F32) for h, cols in shares]
-        for h, cols in shares:
-            nc.gpsimd.tensor_tensor(sized[h][:], probs[h][:, :cols], size_row[:, :cols], ALU.mult)
-        for h, cols in shares:
-            nc.gpsimd.tensor_scalar(weights[h][:, :cols], sized[h][:], inv_total[:, h : h + 1], 0.0, ALU.mult, ALU.add)
-        nc.vector.scalar_tensor_tensor(
-            weights[1][:, split:].rearrange("p (s r) -> p s r", r=PACK),
-            probs[1][:, split:].rearrange("p (s r) -> p s r", r=PACK),
-            inv_total[:, 1:2],
-            size_bank[:].rearrange("p (r s) -> p s r", r=PACK)[:, split // PACK :, :],
-            ALU.mult,
-            ALU.mult,
-        )
-        last = sbuf("gathered3", [P, I], BF16, tag="total")
+        weights = [sbuf("weights0", [P, I], BF16), sbuf("weights1", [P, I], BF16)]
+        for h in range(HALVES):
+            sized = sbuf("sized%d" % h, [P, I], F32)
+            nc.gpsimd.tensor_tensor(sized[:], probs[h], size_row, ALU.mult)
+            nc.gpsimd.tensor_scalar(weights[h][:], sized[:], inv_total[h][:], 0.0, ALU.mult, ALU.add)
+        last = sbuf("gathered3", [P, I], BF16, tag="total1")
         nc.vector.tensor_copy(last[:], pools[3][:].indirect(token_list[:]))
 
         def turn(src, bank, dst):
@@ -146,13 +139,18 @@ def tile_attend_vqattention_pl_kernel(tc, query, book_words, book_scales, size, 
                 nc.tensor.transpose(bank[:, u * P : (u + 1) * P], words[:, u : I // 2 : 2], ident[:])
             nc.scalar.copy(dst.bitcast(F32).rearrange("p (m u) -> p m u", u=2), bank[:, : 2 * P].rearrange("p (u m) -> p m u", u=2))
 
-        grouped = sbuf("grouped", [P, 6 * I], BF16)
-        turn(second[:], banks[0], grouped[:, 3 * I : 4 * I])
-        turn(first[:], banks[1], grouped[:, 2 * I : 3 * I])
-        turn(third, banks[2], grouped[:, 4 * I : 5 * I])
-        turn(weights[0][:], banks[3], grouped[:, :I])
-        turn(weights[1][:], banks[0], grouped[:, I : 2 * I])
-        turn(last[:], banks[1], grouped[:, 5 * I :])
+        grouped = after_cast[:, I:].bitcast(BF16)
+        value_slot = [1, 2, 3, 5]
+        weight_slot = [0, 4]
+        for src, bank, slot in [
+            (second, 0, value_slot[1]),
+            (first[:], 1, value_slot[0]),
+            (third, 2, value_slot[2]),
+            (weights[0][:], 3, weight_slot[0]),
+            (weights[1][:], 0, weight_slot[1]),
+            (last[:], 1, value_slot[3]),
+        ]:
+            turn(src, banks[bank], grouped[:, slot * I : (slot + 1) * I])
         codes = sbuf("codes", [P, 6 * P], U32, tag="pool3")
         planes = sbuf("planes", [P, 6 * P], U8)
         for first_col, cols in [(0, 4 * P), (4 * P, P), (5 * P, P)]:
@@ -169,15 +167,17 @@ def tile_attend_vqattention_pl_kernel(tc, query, book_words, book_scales, size, 
         copies = [nc.vector.tensor_copy, nc.scalar.copy]
 
         def multiply(pair):
-            for n in range(2):
-                t = 2 * pair + n
-                for h in (1, 0):
+            for h in (0, 1) if pair == 0 else (1, 0):
+                w_cols = slice(weight_slot[h] * P, (weight_slot[h] + 1) * P)
+                for n in range(2):
+                    slot = value_slot[2 * pair + n]
+                    v_cols = slice(slot * P, (slot + 1) * P)
                     nc.tensor.matmul_mx(
                         out=out_banks[pair][h][:, n * P : (n + 1) * P],
-                        lhsT=codes[:, (2 + t) * P : (3 + t) * P].bitcast(FP8X4),
-                        lhsT_scale=planes[:, (2 + t) * P : (3 + t) * P],
-                        rhs=codes[:, h * P : (h + 1) * P].bitcast(FP8X4),
-                        rhs_scale=planes[:, h * P : (h + 1) * P],
+                        lhsT=codes[:, v_cols].bitcast(FP8X4),
+                        lhsT_scale=planes[:, v_cols],
+                        rhs=codes[:, w_cols].bitcast(FP8X4),
+                        rhs_scale=planes[:, w_cols],
                         start=True,
                         stop=True,
                     )

@@ -22,6 +22,7 @@ P = 128
 PACK = 4
 BANK = 512
 HALVES = Q // P
+SHARE = 256
 
 
 def tile_attend_vqattention_pl_kernel(tc, query, book_words, book_scales, size, vals, offs, offs2, out_0, out_1, out_2):
@@ -123,13 +124,19 @@ def tile_attend_vqattention_pl_kernel(tc, query, book_words, book_scales, size, 
         nc.scalar.activation(first[:], pool0_bf16[:].indirect(token_list[:]), ACT.Copy)
         nc.vector.tensor_copy(second, pools[1][:].indirect(token_list[:]))
         nc.vector.reciprocal(inv_total[1][:], total[1][:])
+        weights = [sbuf("weights0", [P, I], BF16), sbuf("weights1", [P, I], BF16)]
+        sized = [sbuf("sized%d" % h, [P, I], F32) for h in range(HALVES)]
+        nc.vector.tensor_tensor(
+            sized[1][:, SHARE:].rearrange("p (s r) -> p s r", r=PACK),
+            probs[1][:, SHARE:].rearrange("p (s r) -> p s r", r=PACK),
+            size_bank[:].rearrange("p (r s) -> p s r", r=PACK)[:, SHARE // PACK :, :],
+            ALU.mult,
+        )
         third = sbuf("gathered2", [P, I], BF16)[:]
         nc.vector.tensor_copy(third, pools[2][:].indirect(token_list[:]))
-        weights = [sbuf("weights0", [P, I], BF16), sbuf("weights1", [P, I], BF16)]
-        for h in range(HALVES):
-            sized = sbuf("sized%d" % h, [P, I], F32)
-            nc.gpsimd.tensor_tensor(sized[:], probs[h], size_row, ALU.mult)
-            nc.gpsimd.tensor_scalar(weights[h][:], sized[:], inv_total[h][:], 0.0, ALU.mult, ALU.add)
+        for h, width in enumerate([I, SHARE]):
+            nc.gpsimd.tensor_tensor(sized[h][:, :width], probs[h][:, :width], size_row[:, :width], ALU.mult)
+            nc.gpsimd.tensor_scalar(weights[h][:], sized[h][:], inv_total[h][:], 0.0, ALU.mult, ALU.add)
         last = sbuf("gathered3", [P, I], BF16, tag="total1")
         nc.vector.tensor_copy(last[:], pools[3][:].indirect(token_list[:]))
 

@@ -147,8 +147,8 @@ def tile_attend_vqattention_pl_kernel(tc, query, book_words, book_scales, size, 
             nc.scalar.copy(dst.bitcast(F32).rearrange("p (m u) -> p m u", u=2), bank[:, : 2 * P].rearrange("p (u m) -> p m u", u=2))
 
         grouped = after_cast[:, I:].bitcast(BF16)
-        value_slot = [1, 2, 3, 5]
-        weight_slot = [0, 4]
+        value_slot = [1, 2, 4, 5]
+        weight_slot = [0, 3]
         for src, bank, slot in [
             (second, 0, value_slot[1]),
             (first[:], 1, value_slot[0]),
@@ -160,7 +160,7 @@ def tile_attend_vqattention_pl_kernel(tc, query, book_words, book_scales, size, 
             turn(src, banks[bank], grouped[:, slot * I : (slot + 1) * I])
         codes = sbuf("codes", [P, 6 * P], U32, tag="pool3")
         planes = sbuf("planes", [P, 6 * P], U8)
-        for first_col, cols in [(0, 4 * P), (4 * P, P), (5 * P, P)]:
+        for first_col, cols in [(0, 2 * P), (2 * P, 2 * P), (4 * P, P), (5 * P, P)]:
             nc.vector.quantize_mx(
                 out=codes[:, first_col : first_col + cols].bitcast(FP8X4),
                 scales=planes[:, first_col : first_col + cols],
@@ -174,9 +174,10 @@ def tile_attend_vqattention_pl_kernel(tc, query, book_words, book_scales, size, 
         copies = [nc.vector.tensor_copy, nc.scalar.copy]
 
         def multiply(pair):
-            for h in (0, 1) if pair == 0 else (1, 0):
+            order = [(h, n) for h in range(2) for n in range(2)] if pair == 0 else [(h, n) for n in range(2) for h in (1, 0)]
+            for h, n in order:
                 w_cols = slice(weight_slot[h] * P, (weight_slot[h] + 1) * P)
-                for n in range(2):
+                if True:
                     slot = value_slot[2 * pair + n]
                     v_cols = slice(slot * P, (slot + 1) * P)
                     nc.tensor.matmul_mx(

@@ -22,23 +22,30 @@ P = 128
 PACK = 4
 BANK = 512
 HALVES = Q // P
-SHARE = 256
+FIRST = 288
+SHORT = 128
+POOL_BYTES = 4 * T
 
 
 def tile_attend_vqattention_pl_kernel(tc, query, book_words, book_scales, size, vals, offs, offs2, out_0, out_1, out_2):
     nc = tc.nc
     with ExitStack() as ctx:
         sb = ctx.enter_context(tc.tile_pool(name="sb", bufs=1))
+        held = ctx.enter_context(tc.tile_pool(name="held", bufs=1))
         ps = ctx.enter_context(tc.psum_pool(name="ps", bufs=1))
 
         def sbuf(name, shape, dtype, tag=None):
             return sb.tile(shape, dtype, name=name, tag=tag or name, align_bytes=64)
+
+        def placed(name, shape, dtype, offset):
+            return held.tile(shape, dtype, name=name, offset=offset, align_bytes=64)
 
         banks = [ps.tile([P, BANK], F32, name="bank%d" % n) for n in range(8)]
 
         query_raw = sbuf("query_raw", [P, PACK, Q], F32)
         book_plane = sbuf("book_plane", [P, C], U8)
         book_codes = sbuf("book_codes", [P, 2 * C], U8)
+        size_cols = sbuf("size_cols", [P, PACK], F32)
         nc.sync.dma_start(out=query_raw[:], in_=query.rearrange("(p j) q -> p j q", j=PACK))
         nc.sync.dma_start(out=book_codes[:].bitcast(I32), in_=book_words[0].bitcast(I32))
         for quad, queue in enumerate([nc.scalar, nc.scalar, nc.sync, nc.scalar]):
@@ -47,18 +54,14 @@ def tile_attend_vqattention_pl_kernel(tc, query, book_words, book_scales, size, 
                 in_=book_scales[0, 4 * quad : 4 * quad + 4, :].bitcast(I32),
             )
         vals_rows = vals.rearrange("(m t) n -> t m n", t=PACK)
-        pool0_parts = [sbuf("pool0_part%d" % n, [P, T // 2], F32) for n in range(2)]
-        pools = {t: sbuf("pool%d" % t, [P, T], F32) for t in range(1, PACK)}
-        size_cols = sbuf("size_cols", [P, PACK], F32)
-        nc.sync.dma_start(out=size_cols[:], in_=size.rearrange("o (s r) -> (o s) r", r=PACK))
-        nc.sync.dma_start(out=pool0_parts[0][:], in_=vals_rows[0][:, : T // 2])
+        pools = [placed("pool%d" % t, [P, T], F32, t * POOL_BYTES) for t in range(PACK)]
         code_list = sbuf("code_list", [P, I // 16], U16)
         nc.sync.dma_start(code_list[:], offs)
-        nc.sync.dma_start(out=pools[1][:], in_=vals_rows[1])
+        nc.sync.dma_start(out=pools[0][:], in_=vals_rows[0])
+        nc.sync.dma_start(out=size_cols[:], in_=size.rearrange("o (s r) -> (o s) r", r=PACK))
         token_list = sbuf("token_list", [P, I // 16], U16)
         nc.sync.dma_start(token_list[:], offs2)
-        nc.sync.dma_start(out=pool0_parts[1][:], in_=vals_rows[0][:, T // 2 :])
-        for t in range(2, PACK):
+        for t in range(1, PACK):
             nc.sync.dma_start(out=pools[t][:], in_=vals_rows[t])
 
         ident = sbuf("ident", [P, P], F32)
@@ -91,132 +94,135 @@ def tile_attend_vqattention_pl_kernel(tc, query, book_words, book_scales, size, 
                 stop=True,
             )
         size_bank = banks[7]
-        pool0_bf16 = sbuf("pool0_bf16", [P, T], BF16, tag="q_grouped1")
-        nc.vector.tensor_copy(pool0_bf16[:, : T // 2], pool0_parts[0][:])
+        for r in range(PACK):
+            nc.tensor.transpose(size_bank[:, r * P : (r + 1) * P], size_cols[:, r : r + 1].to_broadcast([P, P]), ident[:])
+        size_psum = size_bank[:].rearrange("p (r s) -> p s r", r=PACK)
         scores = [sbuf("scores%d" % h, [P, C], F32) for h in range(HALVES)]
         for n, (h, first, width) in enumerate(pieces):
             nc.scalar.copy(scores[h][:, first : first + width], banks[n][:, :width])
-        for r in range(PACK):
-            nc.tensor.transpose(size_bank[:, r * P : (r + 1) * P], size_cols[:, r : r + 1].to_broadcast([P, P]), ident[:])
-        size_row = sbuf("size_row", [P, I], F32)[:]
-        nc.scalar.activation(size_row.rearrange("p (s r) -> p s r", r=PACK), size_bank[:].rearrange("p (r s) -> p s r", r=PACK), ACT.Copy)
 
-        after_size = sbuf("after_size", [P, I + 1], F32, tag="size_cols")
-        picked = [sbuf("picked0", [P, I], F32, tag="pool0_part0")[:], after_size[:, :I]]
-        total = [sbuf("total%d" % h, [P, 1], F32) for h in range(HALVES)]
-        inv_total = [sbuf("inv_total%d" % h, [P, 1], F32) for h in range(HALVES)]
-        neg_max0 = after_size[:, I:]
+        def gather(t, engine, first, last):
+            window = pools[t][:].indirect(token_list[:, first // 16 : last // 16])
+            if engine is nc.vector:
+                nc.vector.tensor_copy(gathered[t][:, first:last], window)
+            else:
+                nc.scalar.activation(gathered[t][:, first:last], window, ACT.Copy)
+
+        picked = [sbuf("picked%d" % h, [P, I], F32)[:] for h in range(HALVES)]
+        probs = [sbuf("probs%d" % h, [P, I], F32)[:] for h in range(HALVES)]
+        total = [sbuf("total%d" % h, [P, 1], F32)[:] for h in range(HALVES)]
+        gathered = [sbuf("gathered%d" % t, [P, I], BF16)[:] for t in range(PACK)]
+        weights = [sbuf("weights%d" % h, [P, I], BF16)[:] for h in range(HALVES)]
+        after_size = sbuf("after_size", [P, 2], F32, tag="size_cols")
+        neg_max = [sbuf("neg_max0", [P, 1], F32)[:], after_size[:, :1]]
         nc.vector.tensor_copy(picked[0], scores[0][:].indirect(code_list[:]))
-        nc.vector.tensor_reduce(neg_max0, picked[0], AXIS.X, ALU.max, negate=True)
-        nc.vector.tensor_copy(picked[1], scores[1][:].indirect(code_list[:]))
-        probs = [sbuf("probs0", [P, I], F32)[:]]
-        nc.scalar.activation(probs[0], picked[0], ACT.Exp, bias=neg_max0, accum_out=total[0][:])
-        nc.vector.reciprocal(inv_total[0][:], total[0][:])
-        after_exp0 = sbuf("after_exp0", [P, I // 2 + 1], F32, tag="pool0_part0")
-        neg_max1 = after_exp0[:, I // 2 :]
-        second = after_exp0[:, : I // 2].bitcast(BF16)
-        nc.vector.tensor_reduce(neg_max1, picked[1], AXIS.X, ALU.max, negate=True)
-        nc.scalar.activation(pool0_bf16[:, T // 2 :], pool0_parts[1][:], ACT.Copy)
-        after_cast = sbuf("after_cast", [P, 4 * I], F32, tag="pool0_part1")
-        probs.append(after_cast[:, :I])
-        nc.scalar.activation(probs[1], picked[1], ACT.Exp, bias=neg_max1, accum_out=total[1][:])
-        first = sbuf("gathered0", [P, I], BF16)
-        nc.scalar.activation(first[:], pool0_bf16[:].indirect(token_list[:]), ACT.Copy)
-        nc.vector.tensor_copy(second, pools[1][:].indirect(token_list[:]))
-        nc.vector.reciprocal(inv_total[1][:], total[1][:])
-        weights = [sbuf("weights0", [P, I], BF16), sbuf("weights1", [P, I], BF16)]
-        sized = [sbuf("sized%d" % h, [P, I], F32) for h in range(HALVES)]
-        nc.vector.tensor_tensor(
-            sized[1][:, SHARE:].rearrange("p (s r) -> p s r", r=PACK),
-            probs[1][:, SHARE:].rearrange("p (s r) -> p s r", r=PACK),
-            size_bank[:].rearrange("p (r s) -> p s r", r=PACK)[:, SHARE // PACK :, :],
-            ALU.mult,
-        )
-        third = sbuf("gathered2", [P, I], BF16)[:]
-        nc.vector.tensor_copy(third, pools[2][:].indirect(token_list[:]))
-        for h, width in enumerate([I, SHARE]):
-            nc.gpsimd.tensor_tensor(sized[h][:, :width], probs[h][:, :width], size_row[:, :width], ALU.mult)
-            nc.gpsimd.tensor_scalar(weights[h][:], sized[h][:], inv_total[h][:], 0.0, ALU.mult, ALU.add)
-        last = sbuf("gathered3", [P, I], BF16, tag="total1")
-        nc.vector.tensor_copy(last[:], pools[3][:].indirect(token_list[:]))
+        nc.scalar.activation(picked[1], scores[1][:].indirect(code_list[:]), ACT.Copy)
+        gather(0, nc.vector, 0, SHORT)
+        gather(0, nc.scalar, SHORT, I)
+        size_row = sbuf("size_row", [P, I], F32)[:]
+        nc.vector.tensor_copy(size_row.rearrange("p (s r) -> p s r", r=PACK), size_psum)
+        for h in range(HALVES):
+            nc.vector.tensor_reduce(neg_max[h], picked[h], AXIS.X, ALU.max, negate=True)
+            nc.scalar.activation(probs[h], picked[h], ACT.Exp, bias=neg_max[h], accum_out=total[h])
+        inv_total = [after_size[:, 1:]]
+        nc.vector.reciprocal(inv_total[0], total[0])
+        gather(1, nc.vector, 0, I)
+        inv_total.append(placed("inv_total1", [P, 1], F32, POOL_BYTES)[:])
+        nc.vector.reciprocal(inv_total[1], total[1])
+        sized = sbuf("sized", [P, I], F32)[:]
+        nc.gpsimd.tensor_tensor(sized, probs[0], size_row, ALU.mult)
+        nc.gpsimd.tensor_scalar(weights[0], sized, inv_total[0], 0.0, ALU.mult, ALU.add)
+        gather(2, nc.scalar, 0, I)
+        gather(3, nc.vector, 0, FIRST)
+        gather(3, nc.scalar, FIRST, I)
 
-        def turn(src, bank, dst):
+        result = [placed("early", [P, 2, Q], F32, 64)[:], sbuf("late", [P, 2, Q], F32)[:]]
+        v_grouped = [
+            placed("v_grouped0", [P, I], BF16, POOL_BYTES + 64)[:],
+            placed("v_grouped1", [P, I], BF16, POOL_BYTES + 64 + 1024)[:],
+            placed("v_grouped2", [P, I], BF16, 3 * POOL_BYTES + 2048)[:],
+            placed("v_grouped3", [P, I], BF16, 2048)[:],
+        ]
+        w_grouped = [placed("w_grouped0", [P, I], BF16, 2 * POOL_BYTES)[:], placed("w_grouped1", [P, I], BF16, 3 * POOL_BYTES + 6144)[:]]
+        o_grouped = [placed("o_grouped%d" % h, [P, P, PACK], BF16, 3008 + 1024 * h) for h in range(HALVES)]
+        v_codes = sbuf("v_codes", [P, PACK * P], U32)
+        w_codes = [placed("w_codes0", [P, P], U32, 3 * POOL_BYTES + 3072)[:], sbuf("w_codes1", [P, P], U32)[:]]
+        v_planes = sbuf("v_planes", [P, PACK * P], U8)
+        w_planes = [sbuf("w_plane%d" % h, [P, P], U8)[:] for h in range(HALVES)]
+
+        def turn(src, bank, dst, copy):
             words = src.bitcast(F32)
             for u in range(2):
                 nc.tensor.transpose(bank[:, u * P : (u + 1) * P], words[:, u : I // 2 : 2], ident[:])
-            nc.scalar.copy(dst.bitcast(F32).rearrange("p (m u) -> p m u", u=2), bank[:, : 2 * P].rearrange("p (u m) -> p m u", u=2))
+            copy(dst.bitcast(F32).rearrange("p (m u) -> p m u", u=2), bank[:, : 2 * P].rearrange("p (u m) -> p m u", u=2))
 
-        grouped = after_cast[:, I:].bitcast(BF16)
-        value_slot = [1, 2, 4, 5]
-        weight_slot = [0, 3]
-        for src, bank, slot in [
-            (second, 0, value_slot[1]),
-            (first[:], 1, value_slot[0]),
-            (third, 2, value_slot[2]),
-            (weights[0][:], 3, weight_slot[0]),
-            (weights[1][:], 0, weight_slot[1]),
-            (last[:], 1, value_slot[3]),
-        ]:
-            turn(src, banks[bank], grouped[:, slot * I : (slot + 1) * I])
-        codes = sbuf("codes", [P, 6 * P], U32, tag="pool3")
-        planes = sbuf("planes", [P, 6 * P], U8)
-        for first_col, cols in [(0, 2 * P), (2 * P, 2 * P), (4 * P, P), (5 * P, P)]:
-            nc.vector.quantize_mx(
-                out=codes[:, first_col : first_col + cols].bitcast(FP8X4),
-                scales=planes[:, first_col : first_col + cols],
-                in_=grouped[:, PACK * first_col : PACK * (first_col + cols)],
-            )
+        def quantise(src, codes, plane):
+            nc.vector.quantize_mx(out=codes.bitcast(FP8X4), scales=plane, in_=src)
 
-        out_banks = [[banks[5], banks[6]], [banks[4], banks[2]]]
-        result = [sbuf("result%d" % pair, [P, 2, Q], F32) for pair in range(2)]
+        out_banks = [[banks[5], banks[6]], [banks[2], banks[3]]]
         out_rows = out_0.rearrange("(m t) q -> m t q", t=PACK)
-        o_grouped = [sbuf("o_grouped%d" % h, [P, P, PACK], BF16) for h in range(HALVES)]
         copies = [nc.vector.tensor_copy, nc.scalar.copy]
 
-        def multiply(pair):
-            order = [(h, n) for h in range(2) for n in range(2)] if pair == 0 else [(h, n) for n in range(2) for h in (1, 0)]
-            for h, n in order:
-                w_cols = slice(weight_slot[h] * P, (weight_slot[h] + 1) * P)
-                if True:
-                    slot = value_slot[2 * pair + n]
-                    v_cols = slice(slot * P, (slot + 1) * P)
-                    nc.tensor.matmul_mx(
-                        out=out_banks[pair][h][:, n * P : (n + 1) * P],
-                        lhsT=codes[:, v_cols].bitcast(FP8X4),
-                        lhsT_scale=planes[:, v_cols],
-                        rhs=codes[:, w_cols].bitcast(FP8X4),
-                        rhs_scale=planes[:, w_cols],
-                        start=True,
-                        stop=True,
-                    )
+        def quantise_values(t):
+            quantise(v_grouped[t], v_codes[:, t * P : (t + 1) * P], v_planes[:, t * P : (t + 1) * P])
 
-        def copy_out(pair, h, copy):
-            copy(result[pair][:, :, h * P : (h + 1) * P], out_banks[pair][h][:, : 2 * P].rearrange("p (t q) -> p t q", t=2))
+        def multiply(t, h):
+            cols = slice(t * P, (t + 1) * P)
+            nc.tensor.matmul_mx(
+                out=out_banks[t // 2][h][:, (t % 2) * P : (t % 2 + 1) * P],
+                lhsT=v_codes[:, cols].bitcast(FP8X4),
+                lhsT_scale=v_planes[:, cols],
+                rhs=w_codes[h].bitcast(FP8X4),
+                rhs_scale=w_planes[h],
+                start=True,
+                stop=True,
+            )
+
+        def copy_out(pair, h):
+            copies[h](result[pair][:, :, h * P : (h + 1) * P], out_banks[pair][h][:, : 2 * P].rearrange("p (t q) -> p t q", t=2))
 
         def group(pair, h):
             copies[h](o_grouped[h][:, :, 2 * pair : 2 * pair + 2], out_banks[pair][h][:, : 2 * P].rearrange("p (t q) -> p q t", t=2))
 
-        multiply(0)
+        turn(gathered[0], banks[0], v_grouped[0], nc.vector.tensor_copy)
+        nc.vector.scalar_tensor_tensor(
+            weights[1].rearrange("p (s r) -> p s r", r=PACK),
+            probs[1].rearrange("p (s r) -> p s r", r=PACK),
+            inv_total[1],
+            size_psum,
+            ALU.mult,
+            ALU.mult,
+        )
+        turn(gathered[1], banks[1], v_grouped[1], nc.vector.tensor_copy)
+        turn(weights[0], banks[0], w_grouped[0], nc.scalar.copy)
+        turn(weights[1], banks[3], w_grouped[1], nc.scalar.copy)
+        quantise_values(0)
+        quantise_values(1)
+        turn(gathered[2], banks[4], v_grouped[2], nc.scalar.copy)
+        turn(gathered[3], banks[1], v_grouped[3], nc.scalar.copy)
         for h in range(HALVES):
-            copy_out(0, h, copies[h])
-        nc.sync.dma_start(out=out_rows[:, :2, :], in_=result[0][:])
+            quantise(w_grouped[h], w_codes[h], w_planes[h])
+        quantise_values(2)
+        quantise_values(3)
         for h in range(HALVES):
+            for t in range(2):
+                multiply(t, h)
+            copy_out(0, h)
             group(0, h)
-        multiply(1)
+        nc.sync.dma_start(out=out_rows[:, :2, :], in_=result[0])
+        for t in range(2, PACK):
+            for h in range(HALVES):
+                multiply(t, h)
         for h in range(HALVES):
             group(1, h)
         for h in range(HALVES):
-            copy_out(1, h, copies[h])
+            copy_out(1, h)
 
         o_codes = sbuf("o_codes", [P, Q], U32)
         o_plane = sbuf("o_plane", [P, Q], U8)
-        for h in (1, 0):
-            nc.vector.quantize_mx(
-                out=o_codes[:, h * P : (h + 1) * P].bitcast(FP8X4),
-                scales=o_plane[:, h * P : (h + 1) * P],
-                in_=o_grouped[h][:].rearrange("p q t -> p (q t)"),
-            )
-        nc.scalar.dma_start(out=out_rows[:, 2:, :], in_=result[1][:])
+        for h in range(HALVES):
+            quantise(o_grouped[h][:].rearrange("p q t -> p (q t)"), o_codes[:, h * P : (h + 1) * P], o_plane[:, h * P : (h + 1) * P])
+        nc.scalar.dma_start(out=out_rows[:, 2:, :], in_=result[1])
         nc.sync.dma_start(out=out_1[0].rearrange("p c r -> p (c r)").bitcast(I32), in_=o_codes[:].bitcast(I32))
         for quad in range(4):
             queue = nc.sync if quad < 2 else nc.scalar

@@ -22,7 +22,7 @@ P = 128
 PACK = 4
 BANK = 512
 HALVES = Q // P
-FIRST = 288
+FIRST = 320
 SHORT = 128
 POOL_BYTES = 4 * T
 
@@ -116,11 +116,11 @@ def tile_attend_vqattention_pl_kernel(tc, query, book_words, book_scales, size, 
         after_size = sbuf("after_size", [P, 2], F32, tag="size_cols")
         neg_max = [sbuf("neg_max0", [P, 1], F32)[:], after_size[:, :1]]
         nc.vector.tensor_copy(picked[0], scores[0][:].indirect(code_list[:]))
-        nc.scalar.activation(picked[1], scores[1][:].indirect(code_list[:]), ACT.Copy)
-        gather(0, nc.vector, 0, SHORT)
-        gather(0, nc.scalar, SHORT, I)
+        nc.scalar.activation(picked[1][:, SHORT:], scores[1][:].indirect(code_list[:, SHORT // 16 :]), ACT.Copy)
+        nc.vector.tensor_copy(picked[1][:, :SHORT], scores[1][:].indirect(code_list[:, : SHORT // 16]))
+        gather(0, nc.scalar, 0, I)
         size_row = sbuf("size_row", [P, I], F32)[:]
-        nc.vector.tensor_copy(size_row.rearrange("p (s r) -> p s r", r=PACK), size_psum)
+        nc.vector.tensor_copy(size_row[:, SHORT:].rearrange("p (s r) -> p s r", r=PACK), size_psum[:, SHORT // PACK :, :])
         for h in range(HALVES):
             nc.vector.tensor_reduce(neg_max[h], picked[h], AXIS.X, ALU.max, negate=True)
             nc.scalar.activation(probs[h], picked[h], ACT.Exp, bias=neg_max[h], accum_out=total[h])
@@ -130,7 +130,13 @@ def tile_attend_vqattention_pl_kernel(tc, query, book_words, book_scales, size, 
         inv_total.append(placed("inv_total1", [P, 1], F32, POOL_BYTES)[:])
         nc.vector.reciprocal(inv_total[1], total[1])
         sized = sbuf("sized", [P, I], F32)[:]
-        nc.gpsimd.tensor_tensor(sized, probs[0], size_row, ALU.mult)
+        nc.gpsimd.tensor_tensor(sized[:, SHORT:], probs[0][:, SHORT:], size_row[:, SHORT:], ALU.mult)
+        nc.vector.tensor_tensor(
+            sized[:, :SHORT].rearrange("p (s r) -> p s r", r=PACK),
+            probs[0][:, :SHORT].rearrange("p (s r) -> p s r", r=PACK),
+            size_psum[:, : SHORT // PACK, :],
+            ALU.mult,
+        )
         nc.gpsimd.tensor_scalar(weights[0], sized, inv_total[0], 0.0, ALU.mult, ALU.add)
         gather(2, nc.scalar, 0, I)
         gather(3, nc.vector, 0, FIRST)
@@ -145,7 +151,10 @@ def tile_attend_vqattention_pl_kernel(tc, query, book_words, book_scales, size, 
         ]
         w_grouped = [placed("w_grouped0", [P, I], BF16, 2 * POOL_BYTES)[:], placed("w_grouped1", [P, I], BF16, 3 * POOL_BYTES + 6144)[:]]
         o_grouped = [placed("o_grouped%d" % h, [P, P, PACK], BF16, 3008 + 1024 * h) for h in range(HALVES)]
-        v_codes = sbuf("v_codes", [P, PACK * P], U32)
+        v_codes = [
+            placed("v_codes1", [P, P], U32, 3 * POOL_BYTES + 3584)[:] if t == 1 else sbuf("v_codes%d" % t, [P, P], U32)[:]
+            for t in range(PACK)
+        ]
         w_codes = [placed("w_codes0", [P, P], U32, 3 * POOL_BYTES + 3072)[:], sbuf("w_codes1", [P, P], U32)[:]]
         v_planes = sbuf("v_planes", [P, PACK * P], U8)
         w_planes = [sbuf("w_plane%d" % h, [P, P], U8)[:] for h in range(HALVES)]
@@ -164,13 +173,13 @@ def tile_attend_vqattention_pl_kernel(tc, query, book_words, book_scales, size, 
         copies = [nc.vector.tensor_copy, nc.scalar.copy]
 
         def quantise_values(t):
-            quantise(v_grouped[t], v_codes[:, t * P : (t + 1) * P], v_planes[:, t * P : (t + 1) * P])
+            quantise(v_grouped[t], v_codes[t], v_planes[:, t * P : (t + 1) * P])
 
         def multiply(t, h):
             cols = slice(t * P, (t + 1) * P)
             nc.tensor.matmul_mx(
                 out=out_banks[t // 2][h][:, (t % 2) * P : (t % 2 + 1) * P],
-                lhsT=v_codes[:, cols].bitcast(FP8X4),
+                lhsT=v_codes[t].bitcast(FP8X4),
                 lhsT_scale=v_planes[:, cols],
                 rhs=w_codes[h].bitcast(FP8X4),
                 rhs_scale=w_planes[h],
@@ -197,11 +206,11 @@ def tile_attend_vqattention_pl_kernel(tc, query, book_words, book_scales, size, 
         turn(weights[0], banks[0], w_grouped[0], nc.scalar.copy)
         turn(weights[1], banks[3], w_grouped[1], nc.scalar.copy)
         quantise_values(0)
-        quantise_values(1)
         turn(gathered[2], banks[4], v_grouped[2], nc.scalar.copy)
         turn(gathered[3], banks[1], v_grouped[3], nc.scalar.copy)
-        for h in range(HALVES):
-            quantise(w_grouped[h], w_codes[h], w_planes[h])
+        quantise(w_grouped[0], w_codes[0], w_planes[0])
+        quantise_values(1)
+        quantise(w_grouped[1], w_codes[1], w_planes[1])
         quantise_values(2)
         quantise_values(3)
         for h in range(HALVES):

@@ -222,19 +222,19 @@ def tile_attend_vqattention_pl_kernel(tc, query, book_words, book_scales, size, 
         for t in range(2, PACK):
             for h in range(HALVES):
                 multiply(t, h)
-        for h in range(HALVES):
-            group(1, h)
-        for h in range(HALVES):
-            copy_out(1, h)
+        group(1, 0)
+        copy_out(1, 0)
+        copy_out(1, 1)
+        group(1, 1)
 
+        nc.sync.dma_start(out=out_rows[:, 2:, :], in_=result[1])
         o_codes = sbuf("o_codes", [P, Q], U32)
         o_plane = sbuf("o_plane", [P, Q], U8)
         for h in range(HALVES):
             quantise(o_grouped[h][:].rearrange("p q t -> p (q t)"), o_codes[:, h * P : (h + 1) * P], o_plane[:, h * P : (h + 1) * P])
-        nc.scalar.dma_start(out=out_rows[:, 2:, :], in_=result[1])
         nc.sync.dma_start(out=out_1[0].rearrange("p c r -> p (c r)").bitcast(I32), in_=o_codes[:].bitcast(I32))
         for quad in range(4):
-            queue = nc.sync if quad < 2 else nc.scalar
+            queue = nc.sync if quad < 1 else nc.scalar
             queue.dma_start(
                 out=out_2[0, 4 * quad : 4 * quad + 4, :].bitcast(I32),
                 in_=o_plane[32 * quad : 32 * quad + 4, :].bitcast(I32),

@@ -222,15 +222,14 @@ def tile_attend_vqattention_pl_kernel(tc, query, book_words, book_scales, size, 
         for t in range(2, PACK):
             for h in range(HALVES):
                 multiply(t, h)
-        group(1, 0)
-        copy_out(1, 0)
-        copy_out(1, 1)
-        group(1, 1)
+        for h in range(HALVES):
+            copy_out(1, h)
+            group(1, h)
 
         nc.sync.dma_start(out=out_rows[:, 2:, :], in_=result[1])
         o_codes = sbuf("o_codes", [P, Q], U32)
         o_plane = sbuf("o_plane", [P, Q], U8)
-        for h in range(HALVES):
+        for h in (1, 0):
             quantise(o_grouped[h][:].rearrange("p q t -> p (q t)"), o_codes[:, h * P : (h + 1) * P], o_plane[:, h * P : (h + 1) * P])
         nc.sync.dma_start(out=out_1[0].rearrange("p c r -> p (c r)").bitcast(I32), in_=o_codes[:].bitcast(I32))
         for quad in range(4):

@@ -21,10 +21,16 @@ AXIS = mybir.AxisListType
 P = 128
 PACK = 4
 BANK = 512
+LIST_ROWS = 16
 HALVES = Q // P
-FIRST = 320
-SHORT = 128
 POOL_BYTES = 4 * T
+GROUPED_BYTES = 2 * I
+ALIGN = 64
+
+VECTOR_LAST_SLOTS = 288
+VECTOR_SCORE_SLOTS = 128
+VECTOR_SIZE_SLOTS = 128
+VECTOR_QUERY_ROWS = 88
 
 
 def tile_attend_vqattention_pl_kernel(tc, query, book_words, book_scales, size, vals, offs, offs2, out_0, out_1, out_2):
@@ -35,10 +41,10 @@ def tile_attend_vqattention_pl_kernel(tc, query, book_words, book_scales, size, 
         ps = ctx.enter_context(tc.psum_pool(name="ps", bufs=1))
 
         def sbuf(name, shape, dtype, tag=None):
-            return sb.tile(shape, dtype, name=name, tag=tag or name, align_bytes=64)
+            return sb.tile(shape, dtype, name=name, tag=tag or name, align_bytes=ALIGN)
 
-        def placed(name, shape, dtype, offset):
-            return held.tile(shape, dtype, name=name, offset=offset, align_bytes=64)
+        def on_pool(t, name, shape, dtype, offset=0):
+            return held.tile(shape, dtype, name=name, offset=t * POOL_BYTES + offset, align_bytes=ALIGN)
 
         banks = [ps.tile([P, BANK], F32, name="bank%d" % n) for n in range(8)]
 
@@ -47,19 +53,19 @@ def tile_attend_vqattention_pl_kernel(tc, query, book_words, book_scales, size, 
         book_codes = sbuf("book_codes", [P, 2 * C], U8)
         size_cols = sbuf("size_cols", [P, PACK], F32)
         nc.sync.dma_start(out=query_raw[:], in_=query.rearrange("(p j) q -> p j q", j=PACK))
-        nc.sync.dma_start(out=book_codes[:].bitcast(I32), in_=book_words[0].bitcast(I32))
-        for quad, queue in enumerate([nc.scalar, nc.scalar, nc.sync, nc.scalar]):
+        for quad, queue in enumerate([nc.scalar, nc.scalar, nc.sync, nc.sync]):
             queue.dma_start(
                 out=book_plane[32 * quad : 32 * quad + 4, :].bitcast(I32),
                 in_=book_scales[0, 4 * quad : 4 * quad + 4, :].bitcast(I32),
             )
+        nc.sync.dma_start(out=book_codes[:].bitcast(I32), in_=book_words[0].bitcast(I32))
         vals_rows = vals.rearrange("(m t) n -> t m n", t=PACK)
-        pools = [placed("pool%d" % t, [P, T], F32, t * POOL_BYTES) for t in range(PACK)]
-        code_list = sbuf("code_list", [P, I // 16], U16)
+        pools = [on_pool(t, "pool%d" % t, [P, T], F32) for t in range(PACK)]
+        code_list = sbuf("code_list", [P, I // LIST_ROWS], U16)
         nc.sync.dma_start(code_list[:], offs)
         nc.sync.dma_start(out=pools[0][:], in_=vals_rows[0])
         nc.sync.dma_start(out=size_cols[:], in_=size.rearrange("o (s r) -> (o s) r", r=PACK))
-        token_list = sbuf("token_list", [P, I // 16], U16)
+        token_list = sbuf("token_list", [P, I // LIST_ROWS], U16)
         nc.sync.dma_start(token_list[:], offs2)
         for t in range(1, PACK):
             nc.sync.dma_start(out=pools[t][:], in_=vals_rows[t])
@@ -73,7 +79,8 @@ def tile_attend_vqattention_pl_kernel(tc, query, book_words, book_scales, size, 
             dst = q_grouped[h].rearrange("p (q j) -> p q j", j=PACK)
             src = query_raw[:, :, h * P : (h + 1) * P].rearrange("p j q -> p q j")
             if h == 0:
-                nc.vector.tensor_copy(dst, src)
+                nc.vector.tensor_copy(dst[:, :VECTOR_QUERY_ROWS, :], src[:, :VECTOR_QUERY_ROWS, :])
+                nc.scalar.activation(dst[:, VECTOR_QUERY_ROWS:, :], src[:, VECTOR_QUERY_ROWS:, :], ACT.Copy)
             else:
                 nc.scalar.activation(dst, src, ACT.Copy)
             codes = sbuf("q_codes%d" % h, [P, P], U32)
@@ -101,12 +108,15 @@ def tile_attend_vqattention_pl_kernel(tc, query, book_words, book_scales, size, 
         for n, (h, first, width) in enumerate(pieces):
             nc.scalar.copy(scores[h][:, first : first + width], banks[n][:, :width])
 
-        def gather(t, engine, first, last):
-            window = pools[t][:].indirect(token_list[:, first // 16 : last // 16])
+        def gather(engine, dst, window, entries, first, last):
+            src = window[:].indirect(entries[:, first // LIST_ROWS : last // LIST_ROWS])
             if engine is nc.vector:
-                nc.vector.tensor_copy(gathered[t][:, first:last], window)
+                nc.vector.tensor_copy(dst[:, first:last], src)
             else:
-                nc.scalar.activation(gathered[t][:, first:last], window, ACT.Copy)
+                nc.scalar.activation(dst[:, first:last], src, ACT.Copy)
+
+        def by_word(ap):
+            return ap.rearrange("p (s r) -> p s r", r=PACK)
 
         picked = [sbuf("picked%d" % h, [P, I], F32)[:] for h in range(HALVES)]
         probs = [sbuf("probs%d" % h, [P, I], F32)[:] for h in range(HALVES)]
@@ -115,55 +125,61 @@ def tile_attend_vqattention_pl_kernel(tc, query, book_words, book_scales, size, 
         weights = [sbuf("weights%d" % h, [P, I], BF16)[:] for h in range(HALVES)]
         after_size = sbuf("after_size", [P, 2], F32, tag="size_cols")
         neg_max = [sbuf("neg_max0", [P, 1], F32)[:], after_size[:, :1]]
-        nc.vector.tensor_copy(picked[0], scores[0][:].indirect(code_list[:]))
-        nc.scalar.activation(picked[1][:, SHORT:], scores[1][:].indirect(code_list[:, SHORT // 16 :]), ACT.Copy)
-        nc.vector.tensor_copy(picked[1][:, :SHORT], scores[1][:].indirect(code_list[:, : SHORT // 16]))
-        gather(0, nc.scalar, 0, I)
+        gather(nc.vector, picked[0], scores[0], code_list, 0, I)
+        gather(nc.scalar, picked[1], scores[1], code_list, VECTOR_SCORE_SLOTS, I)
+        gather(nc.vector, picked[1], scores[1], code_list, 0, VECTOR_SCORE_SLOTS)
+        gather(nc.scalar, gathered[0], pools[0], token_list, 0, I)
         size_row = sbuf("size_row", [P, I], F32)[:]
-        nc.vector.tensor_copy(size_row[:, SHORT:].rearrange("p (s r) -> p s r", r=PACK), size_psum[:, SHORT // PACK :, :])
+        nc.vector.tensor_copy(by_word(size_row[:, VECTOR_SIZE_SLOTS:]), size_psum[:, VECTOR_SIZE_SLOTS // PACK :, :])
         for h in range(HALVES):
             nc.vector.tensor_reduce(neg_max[h], picked[h], AXIS.X, ALU.max, negate=True)
             nc.scalar.activation(probs[h], picked[h], ACT.Exp, bias=neg_max[h], accum_out=total[h])
         inv_total = [after_size[:, 1:]]
         nc.vector.reciprocal(inv_total[0], total[0])
-        gather(1, nc.vector, 0, I)
-        inv_total.append(placed("inv_total1", [P, 1], F32, POOL_BYTES)[:])
+        gather(nc.vector, gathered[1], pools[1], token_list, 0, I)
+        inv_total.append(on_pool(1, "inv_total1", [P, 1], F32)[:])
         nc.vector.reciprocal(inv_total[1], total[1])
         sized = sbuf("sized", [P, I], F32)[:]
-        nc.gpsimd.tensor_tensor(sized[:, SHORT:], probs[0][:, SHORT:], size_row[:, SHORT:], ALU.mult)
+        nc.gpsimd.tensor_tensor(
+            sized[:, VECTOR_SIZE_SLOTS:], probs[0][:, VECTOR_SIZE_SLOTS:], size_row[:, VECTOR_SIZE_SLOTS:], ALU.mult
+        )
         nc.vector.tensor_tensor(
-            sized[:, :SHORT].rearrange("p (s r) -> p s r", r=PACK),
-            probs[0][:, :SHORT].rearrange("p (s r) -> p s r", r=PACK),
-            size_psum[:, : SHORT // PACK, :],
+            by_word(sized[:, :VECTOR_SIZE_SLOTS]),
+            by_word(probs[0][:, :VECTOR_SIZE_SLOTS]),
+            size_psum[:, : VECTOR_SIZE_SLOTS // PACK, :],
             ALU.mult,
         )
         nc.gpsimd.tensor_scalar(weights[0], sized, inv_total[0], 0.0, ALU.mult, ALU.add)
-        gather(2, nc.scalar, 0, I)
-        gather(3, nc.vector, 0, FIRST)
-        gather(3, nc.scalar, FIRST, I)
+        gather(nc.scalar, gathered[2], pools[2], token_list, 0, I)
+        gather(nc.vector, gathered[3], pools[3], token_list, 0, VECTOR_LAST_SLOTS)
+        gather(nc.scalar, gathered[3], pools[3], token_list, VECTOR_LAST_SLOTS, I)
 
-        result = [placed("early", [P, 2, Q], F32, 64)[:], sbuf("late", [P, 2, Q], F32)[:]]
+        last_at = 2 * GROUPED_BYTES
+        grouped_at = last_at + GROUPED_BYTES - ALIGN
+        result = [sbuf("early", [P, 2, Q], F32)[:], sbuf("late", [P, 2, Q], F32)[:]]
         v_grouped = [
-            placed("v_grouped0", [P, I], BF16, POOL_BYTES + 64)[:],
-            placed("v_grouped1", [P, I], BF16, POOL_BYTES + 64 + 1024)[:],
-            placed("v_grouped2", [P, I], BF16, 3 * POOL_BYTES + 2048)[:],
-            placed("v_grouped3", [P, I], BF16, 2048)[:],
+            on_pool(1, "v_grouped0", [P, I], BF16, ALIGN)[:],
+            on_pool(1, "v_grouped1", [P, I], BF16, ALIGN + GROUPED_BYTES)[:],
+            on_pool(3, "v_grouped2", [P, I], BF16, 2 * GROUPED_BYTES)[:],
+            on_pool(0, "v_grouped3", [P, I], BF16, last_at)[:],
         ]
-        w_grouped = [placed("w_grouped0", [P, I], BF16, 2 * POOL_BYTES)[:], placed("w_grouped1", [P, I], BF16, 3 * POOL_BYTES + 6144)[:]]
-        o_grouped = [placed("o_grouped%d" % h, [P, P, PACK], BF16, 3008 + 1024 * h) for h in range(HALVES)]
-        v_codes = [
-            placed("v_codes1", [P, P], U32, 3 * POOL_BYTES + 3584)[:] if t == 1 else sbuf("v_codes%d" % t, [P, P], U32)[:]
-            for t in range(PACK)
-        ]
-        w_codes = [placed("w_codes0", [P, P], U32, 3 * POOL_BYTES + 3072)[:], sbuf("w_codes1", [P, P], U32)[:]]
+        w_grouped = [on_pool(2, "w_grouped0", [P, I], BF16)[:], on_pool(3, "w_grouped1", [P, I], BF16, 6 * GROUPED_BYTES)[:]]
+        o_grouped = [on_pool(0, "o_grouped%d" % h, [P, P, PACK], BF16, grouped_at + GROUPED_BYTES * h) for h in range(HALVES)]
+        v_codes = [sbuf("v_codes%d" % t, [P, P], U32)[:] for t in range(PACK)]
+        w_codes = [on_pool(3, "w_codes0", [P, P], U32, 3 * GROUPED_BYTES)[:], sbuf("w_codes1", [P, P], U32)[:]]
         v_planes = sbuf("v_planes", [P, PACK * P], U8)
         w_planes = [sbuf("w_plane%d" % h, [P, P], U8)[:] for h in range(HALVES)]
 
-        def turn(src, bank, dst, copy):
+        def turn(src, bank, dst, copy, parts=1):
             words = src.bitcast(F32)
             for u in range(2):
                 nc.tensor.transpose(bank[:, u * P : (u + 1) * P], words[:, u : I // 2 : 2], ident[:])
-            copy(dst.bitcast(F32).rearrange("p (m u) -> p m u", u=2), bank[:, : 2 * P].rearrange("p (u m) -> p m u", u=2))
+            for row in range(0, P, P // parts):
+                rows = slice(row, row + P // parts)
+                copy(
+                    dst.bitcast(F32).rearrange("p (m u) -> p m u", u=2)[:, rows, :],
+                    bank[:, : 2 * P].rearrange("p (u m) -> p m u", u=2)[:, rows, :],
+                )
 
         def quantise(src, codes, plane):
             nc.vector.quantize_mx(out=codes.bitcast(FP8X4), scales=plane, in_=src)
@@ -172,68 +188,58 @@ def tile_attend_vqattention_pl_kernel(tc, query, book_words, book_scales, size, 
         out_rows = out_0.rearrange("(m t) q -> m t q", t=PACK)
         copies = [nc.vector.tensor_copy, nc.scalar.copy]
 
-        def quantise_values(t):
-            quantise(v_grouped[t], v_codes[t], v_planes[:, t * P : (t + 1) * P])
+        def quantise_values(t, parts=1):
+            for row in range(0, P, P // parts):
+                end = row + P // parts
+                quantise(v_grouped[t][:, PACK * row : PACK * end], v_codes[t][:, row:end], v_planes[:, t * P + row : t * P + end])
 
         def multiply(t, h):
-            cols = slice(t * P, (t + 1) * P)
             nc.tensor.matmul_mx(
                 out=out_banks[t // 2][h][:, (t % 2) * P : (t % 2 + 1) * P],
                 lhsT=v_codes[t].bitcast(FP8X4),
-                lhsT_scale=v_planes[:, cols],
+                lhsT_scale=v_planes[:, t * P : (t + 1) * P],
                 rhs=w_codes[h].bitcast(FP8X4),
                 rhs_scale=w_planes[h],
                 start=True,
                 stop=True,
             )
 
-        def copy_out(pair, h):
-            copies[h](result[pair][:, :, h * P : (h + 1) * P], out_banks[pair][h][:, : 2 * P].rearrange("p (t q) -> p t q", t=2))
-
-        def group(pair, h):
-            copies[h](o_grouped[h][:, :, 2 * pair : 2 * pair + 2], out_banks[pair][h][:, : 2 * P].rearrange("p (t q) -> p q t", t=2))
+        def empty_bank(pair, h, float_copy):
+            sums = out_banks[pair][h][:, : 2 * P]
+            float_copy(result[pair][:, :, h * P : (h + 1) * P], sums.rearrange("p (t q) -> p t q", t=2))
+            copies[h](o_grouped[h][:, :, 2 * pair : 2 * pair + 2], sums.rearrange("p (t q) -> p q t", t=2))
 
         turn(gathered[0], banks[0], v_grouped[0], nc.vector.tensor_copy)
-        nc.vector.scalar_tensor_tensor(
-            weights[1].rearrange("p (s r) -> p s r", r=PACK),
-            probs[1].rearrange("p (s r) -> p s r", r=PACK),
-            inv_total[1],
-            size_psum,
-            ALU.mult,
-            ALU.mult,
-        )
+        nc.vector.scalar_tensor_tensor(by_word(weights[1]), by_word(probs[1]), inv_total[1], size_psum, ALU.mult, ALU.mult)
         turn(gathered[1], banks[1], v_grouped[1], nc.vector.tensor_copy)
         turn(weights[0], banks[0], w_grouped[0], nc.scalar.copy)
         turn(weights[1], banks[3], w_grouped[1], nc.scalar.copy)
         quantise_values(0)
-        turn(gathered[2], banks[4], v_grouped[2], nc.scalar.copy)
-        turn(gathered[3], banks[1], v_grouped[3], nc.scalar.copy)
-        quantise(w_grouped[0], w_codes[0], w_planes[0])
         quantise_values(1)
+        quantise(w_grouped[0], w_codes[0], w_planes[0])
+        turn(gathered[2], banks[4], v_grouped[2], nc.vector.tensor_copy)
+        turn(gathered[3], banks[1], v_grouped[3], nc.scalar.copy, parts=2)
         quantise(w_grouped[1], w_codes[1], w_planes[1])
         quantise_values(2)
-        quantise_values(3)
+        quantise_values(3, parts=2)
         for h in range(HALVES):
             for t in range(2):
                 multiply(t, h)
-            copy_out(0, h)
-            group(0, h)
+            empty_bank(0, h, nc.scalar.copy)
         nc.sync.dma_start(out=out_rows[:, :2, :], in_=result[0])
         for t in range(2, PACK):
             for h in range(HALVES):
                 multiply(t, h)
         for h in range(HALVES):
-            copy_out(1, h)
-            group(1, h)
-
+            empty_bank(1, h, copies[h])
         nc.sync.dma_start(out=out_rows[:, 2:, :], in_=result[1])
+
         o_codes = sbuf("o_codes", [P, Q], U32)
         o_plane = sbuf("o_plane", [P, Q], U8)
         for h in (1, 0):
             quantise(o_grouped[h][:].rearrange("p q t -> p (q t)"), o_codes[:, h * P : (h + 1) * P], o_plane[:, h * P : (h + 1) * P])
         nc.sync.dma_start(out=out_1[0].rearrange("p c r -> p (c r)").bitcast(I32), in_=o_codes[:].bitcast(I32))
-        for quad in range(4):
-            queue = nc.sync if quad < 1 else nc.scalar
+        for quad, queue in enumerate([nc.sync, nc.scalar, nc.scalar, nc.scalar]):
             queue.dma_start(
                 out=out_2[0, 4 * quad : 4 * quad + 4, :].bitcast(I32),
                 in_=o_plane[32 * quad : 32 * quad + 4, :].bitcast(I32),

@@ -27,8 +27,8 @@ POOL_BYTES = 4 * T
 GROUPED_BYTES = 2 * I
 ALIGN = 64
 
-VECTOR_LAST_SLOTS = 288
-VECTOR_SCORE_SLOTS = 128
+VECTOR_LAST_SLOTS = 256
+VECTOR_SCORE_SLOTS = 96
 VECTOR_SIZE_SLOTS = 128
 VECTOR_QUERY_ROWS = 88
 
@@ -89,7 +89,7 @@ def tile_attend_vqattention_pl_kernel(tc, query, book_words, book_scales, size, 
             q_codes.append(codes)
             q_planes.append(plane)
 
-        pieces = [(0, n * 256, 256) for n in range(4)] + [(1, 0, 512), (1, 512, 256), (1, 768, 256)]
+        pieces = [(h, n * 256, 256) for h in range(HALVES) for n in range(4)]
         for n, (h, first, width) in enumerate(pieces):
             nc.tensor.matmul_mx(
                 out=banks[n][:, :width],
@@ -100,13 +100,14 @@ def tile_attend_vqattention_pl_kernel(tc, query, book_words, book_scales, size, 
                 start=True,
                 stop=True,
             )
-        size_bank = banks[7]
+        scores = [sbuf("scores%d" % h, [P, C], F32) for h in range(HALVES)]
+        for n, (h, first, width) in enumerate(pieces):
+            copy = nc.vector.tensor_copy if n in (0, 2) else nc.scalar.copy
+            copy(scores[h][:, first : first + width], banks[n][:, :width])
+        size_bank = banks[0]
         for r in range(PACK):
             nc.tensor.transpose(size_bank[:, r * P : (r + 1) * P], size_cols[:, r : r + 1].to_broadcast([P, P]), ident[:])
         size_psum = size_bank[:].rearrange("p (r s) -> p s r", r=PACK)
-        scores = [sbuf("scores%d" % h, [P, C], F32) for h in range(HALVES)]
-        for n, (h, first, width) in enumerate(pieces):
-            nc.scalar.copy(scores[h][:, first : first + width], banks[n][:, :width])
 
         def gather(engine, dst, window, entries, first, last):
             src = window[:].indirect(entries[:, first // LIST_ROWS : last // LIST_ROWS])
@@ -209,10 +210,10 @@ def tile_attend_vqattention_pl_kernel(tc, query, book_words, book_scales, size, 
             float_copy(result[pair][:, :, h * P : (h + 1) * P], sums.rearrange("p (t q) -> p t q", t=2))
             copies[h](o_grouped[h][:, :, 2 * pair : 2 * pair + 2], sums.rearrange("p (t q) -> p q t", t=2))
 
-        turn(gathered[0], banks[0], v_grouped[0], nc.vector.tensor_copy)
+        turn(gathered[0], banks[7], v_grouped[0], nc.vector.tensor_copy)
         nc.vector.scalar_tensor_tensor(by_word(weights[1]), by_word(probs[1]), inv_total[1], size_psum, ALU.mult, ALU.mult)
         turn(gathered[1], banks[1], v_grouped[1], nc.vector.tensor_copy)
-        turn(weights[0], banks[0], w_grouped[0], nc.scalar.copy)
+        turn(weights[0], banks[7], w_grouped[0], nc.scalar.copy)
         turn(weights[1], banks[3], w_grouped[1], nc.scalar.copy)
         quantise_values(0)
         quantise_values(1)
@@ -225,8 +226,10 @@ def tile_attend_vqattention_pl_kernel(tc, query, book_words, book_scales, size, 
         for h in range(HALVES):
             for t in range(2):
                 multiply(t, h)
-            empty_bank(0, h, nc.scalar.copy)
+            nc.scalar.copy(result[0][:, :, h * P : (h + 1) * P], out_banks[0][h][:, : 2 * P].rearrange("p (t q) -> p t q", t=2))
         nc.sync.dma_start(out=out_rows[:, :2, :], in_=result[0])
+        nc.vector.tensor_copy(o_grouped[0][:, :, :2], result[0][:, :, :P].rearrange("p t q -> p q t"))
+        nc.scalar.copy(o_grouped[1][:, :, :2], out_banks[0][1][:, : 2 * P].rearrange("p (t q) -> p q t", t=2))
         for t in range(2, PACK):
             for h in range(HALVES):
                 multiply(t, h)
@@ -239,7 +242,7 @@ def tile_attend_vqattention_pl_kernel(tc, query, book_words, book_scales, size, 
         for h in (1, 0):
             quantise(o_grouped[h][:].rearrange("p q t -> p (q t)"), o_codes[:, h * P : (h + 1) * P], o_plane[:, h * P : (h + 1) * P])
         nc.sync.dma_start(out=out_1[0].rearrange("p c r -> p (c r)").bitcast(I32), in_=o_codes[:].bitcast(I32))
-        for quad, queue in enumerate([nc.sync, nc.scalar, nc.scalar, nc.scalar]):
+        for quad, queue in enumerate([nc.sync, nc.sync, nc.scalar, nc.scalar]):
             queue.dma_start(
                 out=out_2[0, 4 * quad : 4 * quad + 4, :].bitcast(I32),
                 in_=o_plane[32 * quad : 32 * quad + 4, :].bitcast(I32),

@@ -53,10 +53,10 @@ def tile_attend_vqattention_pl_kernel(tc, query, book_words, book_scales, size, 
         book_codes = sbuf("book_codes", [P, 2 * C], U8)
         size_cols = sbuf("size_cols", [P, PACK], F32)
         nc.sync.dma_start(out=query_raw[:], in_=query.rearrange("(p j) q -> p j q", j=PACK))
-        for quad, queue in enumerate([nc.scalar, nc.scalar, nc.sync, nc.sync]):
+        for row, queue in enumerate([nc.scalar, nc.scalar, nc.sync, nc.sync]):
             queue.dma_start(
-                out=book_plane[32 * quad : 32 * quad + 4, :].bitcast(I32),
-                in_=book_scales[0, 4 * quad : 4 * quad + 4, :].bitcast(I32),
+                out=book_plane[row:P:32, :].bitcast(I32),
+                in_=book_scales[0, row:16:4, :].bitcast(I32),
             )
         nc.sync.dma_start(out=book_codes[:].bitcast(I32), in_=book_words[0].bitcast(I32))
         vals_rows = vals.rearrange("(m t) n -> t m n", t=PACK)

@@ -26,6 +26,7 @@ HALVES = Q // P
 POOL_BYTES = 4 * T
 GROUPED_BYTES = 2 * I
 ALIGN = 64
+BURST = 256
 
 VECTOR_LAST_SLOTS = 256
 VECTOR_SCORE_SLOTS = 96
@@ -40,17 +41,17 @@ def tile_attend_vqattention_pl_kernel(tc, query, book_words, book_scales, size, 
         held = ctx.enter_context(tc.tile_pool(name="held", bufs=1))
         ps = ctx.enter_context(tc.psum_pool(name="ps", bufs=1))
 
-        def sbuf(name, shape, dtype, tag=None):
-            return sb.tile(shape, dtype, name=name, tag=tag or name, align_bytes=ALIGN)
+        def sbuf(name, shape, dtype, tag=None, align=ALIGN):
+            return sb.tile(shape, dtype, name=name, tag=tag or name, align_bytes=align)
 
-        def on_pool(t, name, shape, dtype, offset=0):
-            return held.tile(shape, dtype, name=name, offset=t * POOL_BYTES + offset, align_bytes=ALIGN)
+        def on_pool(t, name, shape, dtype, offset=0, align=ALIGN):
+            return held.tile(shape, dtype, name=name, offset=t * POOL_BYTES + offset, align_bytes=align)
 
         banks = [ps.tile([P, BANK], F32, name="bank%d" % n) for n in range(8)]
 
-        query_raw = sbuf("query_raw", [P, PACK, Q], F32)
-        book_plane = sbuf("book_plane", [P, C], U8)
-        book_codes = sbuf("book_codes", [P, 2 * C], U8)
+        query_raw = sbuf("query_raw", [P, PACK, Q], F32, align=BURST)
+        book_plane = sbuf("book_plane", [P, C], U8, align=BURST)
+        book_codes = sbuf("book_codes", [P, 2 * C], U8, align=BURST)
         size_cols = sbuf("size_cols", [P, PACK], F32)
         nc.sync.dma_start(out=query_raw[:], in_=query.rearrange("(p j) q -> p j q", j=PACK))
         for row, queue in enumerate([nc.scalar, nc.scalar, nc.sync, nc.sync]):
@@ -60,7 +61,7 @@ def tile_attend_vqattention_pl_kernel(tc, query, book_words, book_scales, size, 
             )
         nc.sync.dma_start(out=book_codes[:].bitcast(I32), in_=book_words[0].bitcast(I32))
         vals_rows = vals.rearrange("(m t) n -> t m n", t=PACK)
-        pools = [on_pool(t, "pool%d" % t, [P, T], F32) for t in range(PACK)]
+        pools = [on_pool(t, "pool%d" % t, [P, T], F32, align=BURST) for t in range(PACK)]
         code_list = sbuf("code_list", [P, I // LIST_ROWS], U16)
         nc.sync.dma_start(code_list[:], offs)
         nc.sync.dma_start(out=pools[0][:], in_=vals_rows[0])
@@ -157,7 +158,7 @@ def tile_attend_vqattention_pl_kernel(tc, query, book_words, book_scales, size, 
 
         last_at = 2 * GROUPED_BYTES
         grouped_at = last_at + GROUPED_BYTES - ALIGN
-        result = [sbuf("early", [P, 2, Q], F32)[:], sbuf("late", [P, 2, Q], F32)[:]]
+        result = [sbuf(name, [P, 2, Q], F32, align=BURST)[:] for name in ("early", "late")]
         v_grouped = [
             on_pool(1, "v_grouped0", [P, I], BF16, ALIGN)[:],
             on_pool(1, "v_grouped1", [P, I], BF16, ALIGN + GROUPED_BYTES)[:],
@@ -237,8 +238,8 @@ def tile_attend_vqattention_pl_kernel(tc, query, book_words, book_scales, size, 
             empty_bank(1, h, copies[h])
         nc.sync.dma_start(out=out_rows[:, 2:, :], in_=result[1])
 
-        o_codes = sbuf("o_codes", [P, Q], U32)
-        o_plane = sbuf("o_plane", [P, Q], U8)
+        o_codes = sbuf("o_codes", [P, Q], U32, align=BURST)
+        o_plane = sbuf("o_plane", [P, Q], U8, align=BURST)
         for h in (1, 0):
             quantise(o_grouped[h][:].rearrange("p q t -> p (q t)"), o_codes[:, h * P : (h + 1) * P], o_plane[:, h * P : (h + 1) * P])
         nc.sync.dma_start(out=out_1[0].rearrange("p c r -> p (c r)").bitcast(I32), in_=o_codes[:].bitcast(I32))

@@ -41,7 +41,7 @@ def tile_attend_vqattention_pl_kernel(tc, query, book_words, book_scales, size, 
         held = ctx.enter_context(tc.tile_pool(name="held", bufs=1))
         ps = ctx.enter_context(tc.psum_pool(name="ps", bufs=1))
 
-        def sbuf(name, shape, dtype, tag=None, align=ALIGN):
+        def sbuf(name, shape, dtype, tag=None, align=BURST):
             return sb.tile(shape, dtype, name=name, tag=tag or name, align_bytes=align)
 
         def on_pool(t, name, shape, dtype, offset=0, align=ALIGN):

from contextlib import ExitStack

import concourse.mybir as mybir
from concourse.masks import make_identity

D, C, T, I, Q, E = 512, 1024, 2048, 512, 256, 512
FLOPS = 2 * D * Q * C + 2 * I * E * Q

F32 = mybir.dt.float32
BF16 = mybir.dt.bfloat16
I32 = mybir.dt.int32
U32 = mybir.dt.uint32
U16 = mybir.dt.uint16
U8 = mybir.dt.uint8
FP8X4 = mybir.dt.float8_e4m3fn_x4
FP4X4 = mybir.dt.float4_e2m1fn_x4
ACT = mybir.ActivationFunctionType
ALU = mybir.AluOpType
AXIS = mybir.AxisListType

P = 128
PACK = 4
BANK = 512
LIST_ROWS = 16
HALVES = Q // P
POOL_BYTES = 4 * T
GROUPED_BYTES = 2 * I
ALIGN = 64
BURST = 256

VECTOR_LAST_SLOTS = 256
VECTOR_SCORE_SLOTS = 96
VECTOR_SIZE_SLOTS = 128
VECTOR_QUERY_ROWS = 88


def tile_attend_vqattention_pl_kernel(tc, query, book_words, book_scales, size, vals, offs, offs2, out_0, out_1, out_2):
    nc = tc.nc
    with ExitStack() as ctx:
        sb = ctx.enter_context(tc.tile_pool(name="sb", bufs=1))
        held = ctx.enter_context(tc.tile_pool(name="held", bufs=1))
        ps = ctx.enter_context(tc.psum_pool(name="ps", bufs=1))

        def sbuf(name, shape, dtype, tag=None, align=BURST):
            return sb.tile(shape, dtype, name=name, tag=tag or name, align_bytes=align)

        def on_pool(t, name, shape, dtype, offset=0, align=ALIGN):
            return held.tile(shape, dtype, name=name, offset=t * POOL_BYTES + offset, align_bytes=align)

        banks = [ps.tile([P, BANK], F32, name="bank%d" % n) for n in range(8)]

        query_raw = sbuf("query_raw", [P, PACK, Q], F32, align=BURST)
        book_plane = sbuf("book_plane", [P, C], U8, align=BURST)
        book_codes = sbuf("book_codes", [P, 2 * C], U8, align=BURST)
        size_cols = sbuf("size_cols", [P, PACK], F32)
        nc.sync.dma_start(out=query_raw[:], in_=query.rearrange("(p j) q -> p j q", j=PACK))
        for row, queue in enumerate([nc.scalar, nc.scalar, nc.sync, nc.sync]):
            queue.dma_start(
                out=book_plane[row:P:32, :].bitcast(I32),
                in_=book_scales[0, row:16:4, :].bitcast(I32),
            )
        nc.sync.dma_start(out=book_codes[:].bitcast(I32), in_=book_words[0].bitcast(I32))
        vals_rows = vals.rearrange("(m t) n -> t m n", t=PACK)
        pools = [on_pool(t, "pool%d" % t, [P, T], F32, align=BURST) for t in range(PACK)]
        code_list = sbuf("code_list", [P, I // LIST_ROWS], U16)
        nc.sync.dma_start(code_list[:], offs)
        nc.sync.dma_start(out=pools[0][:], in_=vals_rows[0])
        nc.sync.dma_start(out=size_cols[:], in_=size.rearrange("o (s r) -> (o s) r", r=PACK))
        token_list = sbuf("token_list", [P, I // LIST_ROWS], U16)
        nc.sync.dma_start(token_list[:], offs2)
        for t in range(1, PACK):
            nc.sync.dma_start(out=pools[t][:], in_=vals_rows[t])

        ident = sbuf("ident", [P, P], F32)
        make_identity(nc, ident[:])

        q_codes, q_planes = [], []
        q_grouped = [sbuf("q_grouped%d" % h, [P, P * PACK], BF16)[:] for h in range(HALVES)]
        for h in range(HALVES):
            dst = q_grouped[h].rearrange("p (q j) -> p q j", j=PACK)
            src = query_raw[:, :, h * P : (h + 1) * P].rearrange("p j q -> p q j")
            if h == 0:
                nc.vector.tensor_copy(dst[:, :VECTOR_QUERY_ROWS, :], src[:, :VECTOR_QUERY_ROWS, :])
                nc.scalar.activation(dst[:, VECTOR_QUERY_ROWS:, :], src[:, VECTOR_QUERY_ROWS:, :], ACT.Copy)
            else:
                nc.scalar.activation(dst, src, ACT.Copy)
            codes = sbuf("q_codes%d" % h, [P, P], U32)
            plane = sbuf("q_plane%d" % h, [P, P], U8)
            nc.vector.quantize_mx(out=codes[:].bitcast(FP8X4), scales=plane[:], in_=q_grouped[h])
            q_codes.append(codes)
            q_planes.append(plane)

        pieces = [(h, n * 256, 256) for h in range(HALVES) for n in range(4)]
        for n, (h, first, width) in enumerate(pieces):
            nc.tensor.matmul_mx(
                out=banks[n][:, :width],
                lhsT=q_codes[h][:].bitcast(FP8X4),
                lhsT_scale=q_planes[h][:],
                rhs=book_codes[:, 2 * first : 2 * (first + width)].bitcast(FP4X4),
                rhs_scale=book_plane[:, first : first + width],
                start=True,
                stop=True,
            )
        scores = [sbuf("scores%d" % h, [P, C], F32) for h in range(HALVES)]
        for n, (h, first, width) in enumerate(pieces):
            copy = nc.vector.tensor_copy if n in (0, 2) else nc.scalar.copy
            copy(scores[h][:, first : first + width], banks[n][:, :width])
        size_bank = banks[0]
        for r in range(PACK):
            nc.tensor.transpose(size_bank[:, r * P : (r + 1) * P], size_cols[:, r : r + 1].to_broadcast([P, P]), ident[:])
        size_psum = size_bank[:].rearrange("p (r s) -> p s r", r=PACK)

        def gather(engine, dst, window, entries, first, last):
            src = window[:].indirect(entries[:, first // LIST_ROWS : last // LIST_ROWS])
            if engine is nc.vector:
                nc.vector.tensor_copy(dst[:, first:last], src)
            else:
                nc.scalar.activation(dst[:, first:last], src, ACT.Copy)

        def by_word(ap):
            return ap.rearrange("p (s r) -> p s r", r=PACK)

        picked = [sbuf("picked%d" % h, [P, I], F32)[:] for h in range(HALVES)]
        probs = [sbuf("probs%d" % h, [P, I], F32)[:] for h in range(HALVES)]
        total = [sbuf("total%d" % h, [P, 1], F32)[:] for h in range(HALVES)]
        gathered = [sbuf("gathered%d" % t, [P, I], BF16)[:] for t in range(PACK)]
        weights = [sbuf("weights%d" % h, [P, I], BF16)[:] for h in range(HALVES)]
        after_size = sbuf("after_size", [P, 2], F32, tag="size_cols")
        neg_max = [sbuf("neg_max0", [P, 1], F32)[:], after_size[:, :1]]
        gather(nc.vector, picked[0], scores[0], code_list, 0, I)
        gather(nc.scalar, picked[1], scores[1], code_list, VECTOR_SCORE_SLOTS, I)
        gather(nc.vector, picked[1], scores[1], code_list, 0, VECTOR_SCORE_SLOTS)
        gather(nc.scalar, gathered[0], pools[0], token_list, 0, I)
        size_row = sbuf("size_row", [P, I], F32)[:]
        nc.vector.tensor_copy(by_word(size_row[:, VECTOR_SIZE_SLOTS:]), size_psum[:, VECTOR_SIZE_SLOTS // PACK :, :])
        for h in range(HALVES):
            nc.vector.tensor_reduce(neg_max[h], picked[h], AXIS.X, ALU.max, negate=True)
            nc.scalar.activation(probs[h], picked[h], ACT.Exp, bias=neg_max[h], accum_out=total[h])
        inv_total = [after_size[:, 1:]]
        nc.vector.reciprocal(inv_total[0], total[0])
        gather(nc.vector, gathered[1], pools[1], token_list, 0, I)
        inv_total.append(on_pool(1, "inv_total1", [P, 1], F32)[:])
        nc.vector.reciprocal(inv_total[1], total[1])
        sized = sbuf("sized", [P, I], F32)[:]
        nc.gpsimd.tensor_tensor(
            sized[:, VECTOR_SIZE_SLOTS:], probs[0][:, VECTOR_SIZE_SLOTS:], size_row[:, VECTOR_SIZE_SLOTS:], ALU.mult
        )
        nc.vector.tensor_tensor(
            by_word(sized[:, :VECTOR_SIZE_SLOTS]),
            by_word(probs[0][:, :VECTOR_SIZE_SLOTS]),
            size_psum[:, : VECTOR_SIZE_SLOTS // PACK, :],
            ALU.mult,
        )
        nc.gpsimd.tensor_scalar(weights[0], sized, inv_total[0], 0.0, ALU.mult, ALU.add)
        gather(nc.scalar, gathered[2], pools[2], token_list, 0, I)
        gather(nc.vector, gathered[3], pools[3], token_list, 0, VECTOR_LAST_SLOTS)
        gather(nc.scalar, gathered[3], pools[3], token_list, VECTOR_LAST_SLOTS, I)

        last_at = 2 * GROUPED_BYTES
        grouped_at = last_at + GROUPED_BYTES - ALIGN
        result = [sbuf(name, [P, 2, Q], F32, align=BURST)[:] for name in ("early", "late")]
        v_grouped = [
            on_pool(1, "v_grouped0", [P, I], BF16, ALIGN)[:],
            on_pool(1, "v_grouped1", [P, I], BF16, ALIGN + GROUPED_BYTES)[:],
            on_pool(3, "v_grouped2", [P, I], BF16, 2 * GROUPED_BYTES)[:],
            on_pool(0, "v_grouped3", [P, I], BF16, last_at)[:],
        ]
        w_grouped = [on_pool(2, "w_grouped0", [P, I], BF16)[:], on_pool(3, "w_grouped1", [P, I], BF16, 6 * GROUPED_BYTES)[:]]
        o_grouped = [on_pool(0, "o_grouped%d" % h, [P, P, PACK], BF16, grouped_at + GROUPED_BYTES * h) for h in range(HALVES)]
        v_codes = [sbuf("v_codes%d" % t, [P, P], U32)[:] for t in range(PACK)]
        w_codes = [on_pool(3, "w_codes0", [P, P], U32, 3 * GROUPED_BYTES)[:], sbuf("w_codes1", [P, P], U32)[:]]
        v_planes = sbuf("v_planes", [P, PACK * P], U8)
        w_planes = [sbuf("w_plane%d" % h, [P, P], U8)[:] for h in range(HALVES)]

        def turn(src, bank, dst, copy, parts=1):
            words = src.bitcast(F32)
            for u in range(2):
                nc.tensor.transpose(bank[:, u * P : (u + 1) * P], words[:, u : I // 2 : 2], ident[:])
            for row in range(0, P, P // parts):
                rows = slice(row, row + P // parts)
                copy(
                    dst.bitcast(F32).rearrange("p (m u) -> p m u", u=2)[:, rows, :],
                    bank[:, : 2 * P].rearrange("p (u m) -> p m u", u=2)[:, rows, :],
                )

        def quantise(src, codes, plane):
            nc.vector.quantize_mx(out=codes.bitcast(FP8X4), scales=plane, in_=src)

        out_banks = [[banks[5], banks[6]], [banks[2], banks[3]]]
        out_rows = out_0.rearrange("(m t) q -> m t q", t=PACK)
        copies = [nc.vector.tensor_copy, nc.scalar.copy]

        def quantise_values(t, parts=1):
            for row in range(0, P, P // parts):
                end = row + P // parts
                quantise(v_grouped[t][:, PACK * row : PACK * end], v_codes[t][:, row:end], v_planes[:, t * P + row : t * P + end])

        def multiply(t, h):
            nc.tensor.matmul_mx(
                out=out_banks[t // 2][h][:, (t % 2) * P : (t % 2 + 1) * P],
                lhsT=v_codes[t].bitcast(FP8X4),
                lhsT_scale=v_planes[:, t * P : (t + 1) * P],
                rhs=w_codes[h].bitcast(FP8X4),
                rhs_scale=w_planes[h],
                start=True,
                stop=True,
            )

        def empty_bank(pair, h, float_copy):
            sums = out_banks[pair][h][:, : 2 * P]
            float_copy(result[pair][:, :, h * P : (h + 1) * P], sums.rearrange("p (t q) -> p t q", t=2))
            copies[h](o_grouped[h][:, :, 2 * pair : 2 * pair + 2], sums.rearrange("p (t q) -> p q t", t=2))

        turn(gathered[0], banks[7], v_grouped[0], nc.vector.tensor_copy)
        nc.vector.scalar_tensor_tensor(by_word(weights[1]), by_word(probs[1]), inv_total[1], size_psum, ALU.mult, ALU.mult)
        turn(gathered[1], banks[1], v_grouped[1], nc.vector.tensor_copy)
        turn(weights[0], banks[7], w_grouped[0], nc.scalar.copy)
        turn(weights[1], banks[3], w_grouped[1], nc.scalar.copy)
        quantise_values(0)
        quantise_values(1)
        quantise(w_grouped[0], w_codes[0], w_planes[0])
        turn(gathered[2], banks[4], v_grouped[2], nc.vector.tensor_copy)
        turn(gathered[3], banks[1], v_grouped[3], nc.scalar.copy, parts=2)
        quantise(w_grouped[1], w_codes[1], w_planes[1])
        quantise_values(2)
        quantise_values(3, parts=2)
        for h in range(HALVES):
            for t in range(2):
                multiply(t, h)
            nc.scalar.copy(result[0][:, :, h * P : (h + 1) * P], out_banks[0][h][:, : 2 * P].rearrange("p (t q) -> p t q", t=2))
        nc.sync.dma_start(out=out_rows[:, :2, :], in_=result[0])
        nc.vector.tensor_copy(o_grouped[0][:, :, :2], result[0][:, :, :P].rearrange("p t q -> p q t"))
        nc.scalar.copy(o_grouped[1][:, :, :2], out_banks[0][1][:, : 2 * P].rearrange("p (t q) -> p q t", t=2))
        for t in range(2, PACK):
            for h in range(HALVES):
                multiply(t, h)
        for h in range(HALVES):
            empty_bank(1, h, copies[h])
        nc.sync.dma_start(out=out_rows[:, 2:, :], in_=result[1])

        o_codes = sbuf("o_codes", [P, Q], U32, align=BURST)
        o_plane = sbuf("o_plane", [P, Q], U8, align=BURST)
        for h in (1, 0):
            quantise(o_grouped[h][:].rearrange("p q t -> p (q t)"), o_codes[:, h * P : (h + 1) * P], o_plane[:, h * P : (h + 1) * P])
        nc.sync.dma_start(out=out_1[0].rearrange("p c r -> p (c r)").bitcast(I32), in_=o_codes[:].bitcast(I32))
        for quad, queue in enumerate([nc.sync, nc.sync, nc.scalar, nc.scalar]):
            queue.dma_start(
                out=out_2[0, 4 * quad : 4 * quad + 4, :].bitcast(I32),
                in_=o_plane[32 * quad : 32 * quad + 4, :].bitcast(I32),
            )
